import numpy as np, ml_dtypes
CORES = [83,85,87,115,117,119]
N = 6
BF = ml_dtypes.bfloat16
def gentries(a):
    return np.ascontiguousarray(a.reshape(8, 16, -1).transpose(0, 2, 1)).reshape(8, -1)
def gtable(e):
    e = np.asarray(e); return np.ascontiguousarray(e.reshape(8, -1, 16).transpose(0, 2, 1)).reshape(128, -1).astype(np.int32)
W, L, S, ST = 4096, 128, 32, 4
def parts(rng):
    x = rng.integers(0, 64, (N, 8, 16, W)); v = rng.integers(0, W, (N, 8, L, S)); c = rng.integers(0, W, (N, 8, L, S))
    n = np.where(rng.random((N, 8, L)) < 0.4, rng.integers(0, 4, (N, 8, L)), rng.integers(4, S + 1, (N, 8, L)))
    return x, v, c, n, rng.integers(220, 460, (N, 8)), rng.integers(0, 256, (N, 8, 16))
def pack(x, v, c, n, th, w):
    return {"xc": np.ascontiguousarray(x.reshape(N, 128, W)).astype(np.float32).astype(BF), "vl": np.stack([gtable(a.reshape(8, -1)) for a in v]), "cl": np.stack([gtable(a.reshape(8, -1)) for a in c]),
            "ln": np.ascontiguousarray(n).astype(np.int32), "th": np.ascontiguousarray(th.reshape(N, 8, 1)).astype(np.int32), "wt": np.ascontiguousarray(w.reshape(N, 128, 1)).astype(np.int32)}
def setup_inputs(rng):
    return pack(*parts(rng))
def setup_inputs_ties(rng):
    x, v, c, n, th, w = parts(rng)
    x = np.repeat(8 * rng.integers(0, 8, (N, 8, 1, W)), 16, axis=2); up = rng.integers(0, 3, (N, 8, W)) * (rng.random((N, 8, W)) < 0.4)
    x = x + up[:, :, None, :] * (np.arange(16)[:, None] == rng.integers(0, 16, (N, 8, 1, W)))
    o = np.argsort(rng.random((N, 8)), axis=1); j = o >> 1; less = np.where(rng.random((N, 8)) < 0.6, rng.integers(0, 2, (N, 8)), rng.integers(0, 32, (N, 8)))
    th = np.maximum(128 * j - less, 0); s = np.arange(S)
    for r in range(N):
        z = 128 * int(rng.integers(4, 7))
        for g, e in ((int(np.argmin(o[r])), 0), (int(np.argmax(o[r])), 1)):
            th[r, g] = z + e
            x[r, g, :, 0] = 0; x[r, g, :, 1] = 56; x[r, g, :, 2] = z >> 4; x[r, g, int(rng.integers(0, 16)), 2] += 1
            v[r, g, 1::2] = np.where(s < 2, 0, 2); c[r, g, 1::2] = np.where(s < 1, 1, 2); n[r, g, 1::2] = rng.integers(4, S + 1, L // 2)
    q = int(rng.integers(0, N)); a = (q - 1) % N; b = (q - 2) % N
    n[a] = np.where(n[a] >= 4, rng.integers(4, 6, (8, L)), n[a])
    n[q] = rng.integers(0, 4, (8, L)); p = rng.permutation(8 * L)[:31]; one = rng.integers(0, W, (31, 1))
    n[q, p // L, p % L] = 4; v[q, p // L, p % L] = one; c[q, p // L, p % L] = one; th[q] = 128 * rng.integers(1, 4, 8) - 16
    x[b, :, :, 16:40:3] = 0; x[b, :, :, 17:40:3] = 56; x[b, :, :, 18:40:3] = 63; x[b, :, :, 64:128] = 8 * rng.integers(0, 2, (8, 1, 64))
    f0 = 16 + 3 * (np.arange(L // 4)[:, None] & 7); far = rng.integers(64, 128, (8, L // 4, S)); e = rng.integers(128, W, (8, L // 4, S))
    v[b, :, ::4] = np.where(s == 0, e, np.where((s == 1) | (s >= S - 3), f0 + 2, np.where(s == 2, f0 + 1, far)))
    c[b, :, ::4] = np.where(s == 0, f0 + 2, np.where((s == 1) | (s == S - 3), f0, rng.integers(128, W, far.shape)))
    n[b, :, ::4] = S
    return pack(x, v, c, n, th, w)
def setup_inputs_alike(rng):
    x, v, c, n, th, w = parts(rng)
    few = np.array([0, W - 1, W // 2, 3, W - 2, 17])
    v[:, ::2] = few[rng.integers(0, 6, (N, 4, L, S))]; v[:, 1::2, :, 0] = few[rng.integers(0, 6, (N, 4, L))]
    w[:, ::2] = 0; th[:, ::2] = rng.integers(0, 260, (N, 4)); th[:, 1::2] = rng.integers(150, 500, (N, 4))
    o = rng.permutation(4); shutting = 2 * int(o[0]); taking = 2 * int(o[1]); growing = 1 + 2 * int(rng.integers(0, 4))
    n[:, growing] = rng.integers(4, S + 1, (N, L)); v[:, growing, :, 0] = few[int(rng.integers(0, 6))]; th[:, growing] = 0
    n[:, shutting] = rng.integers(ST + 3, S + 1, (N, L)); th[:, shutting] = 1008
    rest = np.where(rng.random((N, L)) < 0.8, 0, rng.integers(1, 4, (N, L)))
    n[:, taking] = np.where(np.arange(N)[:, None] % 2 == 0, rng.integers(ST + 3, S + 1, (N, L)), rest); th[:, taking] = 1008
    return pack(x, v, c, n, th, w)
def setup_inputs_corners(rng):
    x, v, c, n, th, w = parts(rng)
    lo = (W - 1) * rng.integers(0, 2, (N, 8, 1)); hi = W - 1 - lo
    x[..., 0] = np.where(lo == 0, 0, 63); x[..., W - 1] = np.where(lo == 0, 63, 0)
    n = rng.choice(np.array([0, 1, 2, 3, 4, 5, S - 1, S]), (N, 8, L)); kind = rng.integers(0, 5, (N, 8, L))
    for g, i in ((0, 0), (7, L - 1)):
        n[0, g, i] = S; kind[0, g, i] = 0; n[1, g, i] = 0
    n[N - 1, 7, L - 2] = S; kind[N - 1, 7, L - 2] = 1
    s = np.arange(S); q = np.maximum(n, 4)[..., None]; kd = kind[..., None]; A = lo[..., None]; H = hi[..., None]
    v0 = np.where((s < 2) | (s == q - 1), H, A); v1 = np.where((s == q - 3) | (s == q - 2), H, A); v2 = np.where(s >= q - 3, H, A)
    one = rng.integers(0, W, (N, 8, L, 1))
    v = np.where(kd == 0, v0, np.where(kd == 1, v1, np.where(kd == 2, v2, np.where(kd == 3, one, v))))
    c = np.where(kd < 3, A, np.where(kd == 3, one, c))
    v = np.where(s < n[..., None], v, (W - 1) * rng.integers(0, 2, v.shape)); c = np.where(s < n[..., None], c, (W - 1) * rng.integers(0, 2, c.shape))
    return pack(x, v, c, n, np.array([0, 5, 500, 900])[np.argsort(rng.random((N, 8)), axis=1) >> 1], w)
def setup_inputs_ends(rng):
    x, v, c, n, th, w = parts(rng)
    e = 63 * rng.integers(0, 2, (N, 8, 1)); e[N - 1, 7] = 0
    x = 63 * rng.integers(0, 2, (N, 8, 16, W)); x[..., 0] = e; x[..., W - 1] = 63 - e
    for j in range(1, 17):
        for col in (j, W - 1 - j):
            x[..., col] = 63 - e; x[:, :, j - 1, col] = np.abs(62 - e[..., 0])
    v = np.where(rng.random(v.shape) < 0.75, (W - 1) * rng.integers(0, 2, v.shape), v); c = np.where(rng.random(c.shape) < 0.75, (W - 1) * rng.integers(0, 2, c.shape), c)
    kind = rng.integers(0, 3, (N, 8, L)); kind[..., 0] = 1; kind[..., L - 1] = 1; kind[..., 1] = 2; kind[..., L - 2] = 2
    k1 = kind == 1; k2 = kind == 2; v[k1 | k2] = W - 1; c[k1] = W - 1
    c = np.where(k2[..., None], (W - 1) * rng.integers(0, 2, c.shape), c)
    near = rng.integers(1, 17, (N, 8, L)); near = np.where(rng.random((N, 8, L)) < 0.5, near, W - 1 - near)
    v[..., 0] = np.where(k1, near, v[..., 0]); c[..., 0] = np.where(k1, 0, c[..., 0]); c[..., S - 3] = np.where(k1 | k2, 0, c[..., S - 3])
    v[..., S - 1] = np.where(k1, (W - 1) * rng.integers(0, 2, (N, 8, L)), v[..., S - 1]); v[N - 1, 7, L - 1, S - 1] = 0
    n = np.where(rng.random((N, 8, L)) < 0.7, S, 0); n[..., 0] = S; n[..., 1] = S; n[..., 2] = 0; n[..., L - 2] = S; n[..., L - 1] = S; n[0, :, L - 1] = 0
    th = 1008 * (np.argsort(rng.random((N, 8)), axis=1) & 1)
    if th[N - 1, 7] > 0: th[N - 1] = 1008 - th[N - 1]
    w = 255 * rng.integers(0, 2, (N, 8, 16)); w[:, 7] = 255; w[:, 0] = 0
    return pack(x, v, c, n, th, w)
def setup_inputs_spread(rng):
    x, v, c, n, th, w = parts(rng)
    x = np.minimum((np.exp2(6.1 * rng.random((N, 8, 1, W))) * rng.random((N, 8, 16, W))).astype(np.int64), 63)
    po = rng.choice(np.array([1.0, 2.0, 4.0]), (N, 8, 1, 1)); v = np.minimum((W * rng.random(v.shape) ** po).astype(np.int64), W - 1); c = np.minimum((W * rng.random(c.shape) ** po[:, ::-1]).astype(np.int64), W - 1)
    n = np.minimum(((S + 1) * rng.random((N, 8, L)) ** rng.choice(np.array([0.5, 1.0, 2.0]), (N, 8, 1))).astype(np.int64), S)
    th = np.minimum(np.exp2(10 * rng.random((N, 8))).astype(np.int64) - 1, 1008); w = np.minimum(np.exp2(8.05 * rng.random((N, 8, 16))).astype(np.int64) - 1, 255)
    return pack(x, v, c, n, th, w)
def check_inputs(d):
    bad = []
    for k, lo, hi in (("xc", 0, 63), ("vl", 0, W - 1), ("cl", 0, W - 1), ("ln", 0, S), ("th", 0, 1008), ("wt", 0, 255)):
        a = np.asarray(d[k]).astype(np.float64)
        if not (np.min(a) >= lo and np.max(a) <= hi): bad.append("range of " + k)
    a = np.asarray(d["xc"]).astype(np.float64)
    if not np.all(np.floor(a) == a): bad.append("xc is not whole")
    return bad
def reference(xc, vl, cl, ln, th, wt):
    X = np.ascontiguousarray(xc.astype(np.float32).astype(np.int32).reshape(N, 8, 16, W).transpose(0, 1, 3, 2))
    V = np.stack([gentries(q) for q in vl]).astype(np.int32).reshape(N, 8, L, S); C = np.stack([gentries(q) for q in cl]).astype(np.int32).reshape(N, 8, L, S)
    n = ln.astype(np.int64).reshape(N, 8, L); lim = th.astype(np.int64).reshape(N, 8, 1, 1); w = wt.astype(np.int64).reshape(N, 8, 1, 16)
    a = np.arange(N)[:, None, None, None]; b = np.arange(8)[None, :, None, None]; s = np.arange(S); shut = np.zeros(N, np.int64)
    for t in range(ST):
        XV = X[a, b, V]; XC = X[a, b, C]; live = n >= 4
        bend = np.add.reduce(np.abs(XV[:, :, :, :-1] + XV[:, :, :, 1:] - 2 * XC[:, :, :, :-1]), axis=-1, dtype=np.int32)
        k = np.argmax(np.where(s[:-1] <= n[..., None] - 3, bend, -1), axis=3)[..., None]
        Vk = np.take_along_axis(V, k, 3); Vn = np.take_along_axis(V, k + 1, 3); Ck = np.take_along_axis(C, k, 3)
        y = np.clip(X[a, b, Vk] + X[a, b, Vn] - X[a, b, Ck], 0, 63)
        dist = np.add.reduce(np.abs(XV - y), axis=-1, dtype=np.int32)
        fit = (s >= k + 2) & (s <= n[..., None] - 1) & (dist <= lim + shut[:, None, None, None]) & live[..., None]
        close = np.any(fit, axis=3); m = np.argmax(fit, axis=3)[..., None]; grow = live & ~close
        size = np.where(close[..., None], m - k - 1, 0)
        ix = np.minimum(k + 1 + s, S - 1); keep = s < size
        PV = np.where(keep, np.take_along_axis(V, ix, 3), 0); PC = np.where(keep, np.take_along_axis(C, ix, 3), 0)
        y = y[:, :, :, 0]; u = np.add.reduce(w * y, axis=-1) & (W - 1)
        h = (((u * u) >> 5) + 37 * Vk[..., 0].astype(np.int64)) & (W - 1)
        src = np.minimum(np.where(s <= k, s, s + size - grow[..., None].astype(np.int64)), S - 1)
        V2 = np.take_along_axis(V, src, 3); C2 = np.take_along_axis(C, src, 3); new = grow[..., None] & (s == k + 1)
        V2 = np.where(new, h[..., None], V2); C2 = np.where(new, Vk, np.where(live[..., None] & (s == k), Vn, C2))
        n2 = np.minimum(n + grow.astype(np.int64), S) - size[..., 0]
        for i in range(L - 1, -1, -1):
            p, q = np.nonzero(grow[:, :, i]); X[p, q, h[p, q, i]] = y[p, q, i]
        d = 1 + t % (N - 1)
        came = np.roll(size, d, axis=0)[..., 0]; yin = np.roll(y, d, axis=0); lin = np.roll(live, d, axis=0)
        take = ~live & (came > n)
        V = np.where(take[..., None], np.roll(PV, d, axis=0), V2); C = np.where(take[..., None], np.roll(PC, d, axis=0), C2); n = np.where(take, came, n2)
        V = np.where(s < n[..., None], V, 0).astype(np.int32); C = np.where(s < n[..., None], C, 0).astype(np.int32)
        has = lin & (n >= 1); old = X.copy()
        for i in range(L - 1, -1, -1):
            p, q = np.nonzero(has[:, :, i]); z = V[p, q, i, 0]; X[p, q, z] = (old[p, q, z] + yin[p, q, i]) >> 1
        shut = np.add.reduce(close.astype(np.int64).reshape(N, -1), axis=1) & 31
    return {"yx": np.ascontiguousarray(X.transpose(0, 1, 3, 2)).reshape(N, 128, W).astype(np.float32).astype(BF), "yv": np.stack([gtable(q.reshape(8, -1)) for q in V]).astype(np.float32),
            "yc": np.stack([gtable(q.reshape(8, -1)) for q in C]).astype(np.float32), "yn": n.astype(np.float32)}

@@ -1,0 +1,638 @@
+import numpy as np
+import comms_topo
+from concourse.mybir import dt, AluOpType, AxisListType, ActivationFunctionType
+
+A = AluOpType
+AF = ActivationFunctionType
+N = 6
+ST = 4
+BIG = 16777216
+NX = 4224
+
+SCRATCH = {}
+
+
+def _add(where, dtype, names, cols, rows=128):
+    for nm in names.split():
+        SCRATCH[nm] = (where, [rows, cols], dtype)
+
+
+_add("sbuf", "bfloat16", "X", NX)
+_add("sbuf", "bfloat16", "XV H D AB", 4480)
+_add("sbuf", "int32", "W0 W1 W2 W3 W4 LW0 LW1 LW2 LW3 VI CI DLT BIT", 288)
+_add("sbuf", "bfloat16", "R0 R1 R2 R3 R4 QT ZERO ONES DUPM INV MK RB", 288)
+_add("sbuf", "float32", "POS Z Z0 DW RQ LX OA SP GG PZ WA RA CV E T1 TM RX PP U TDB", 288)
+_add("sbuf", "uint16", "VL CL", 288)
+_add("sbuf", "uint16", "JL OL OB", 8)
+_add("sbuf", "bfloat16", "YR0 YR1 YR2 YR3 LY0 LY1 LY2 LY3", 416)
+_add("sbuf", "float32", "M0 M1 M2 M3 LM0 LM1 LM2 LM3", 24)
+_add("sbuf", "float32", "SM", 720)
+_add("sbuf", "int32", "SI", 240)
+_add("sbuf", "float32", "ROWI", 143)
+_add("sbuf", "bfloat16", "WB1 WBK WB4 WBM WBW", 143)
+_add("sbuf", "bfloat16", "ID IDM IDN DK TK BI YX", 128)
+_add("sbuf", "float32", "BLK GB EX", 128)
+_add("sbuf", "int32", "CIO BO", 128)
+_add("sbuf", "float32", "BS", 128)
+_add("sbuf", "float32", "DG", 16)
+_add("sbuf", "float32", "AA", 1024)
+_add("sbuf", "int32", "VR CR", 256)
+_add("sbuf", "float32", "RT RU TA TB TC TE OUT", 256)
+_add("sbuf", "float32", "OV OC", 256)
+_add("sbuf", "int32", "OI", 256)
+_add("sbuf", "int32", "NR", 8)
+_add("sbuf", "int32", "THR8", 1, 8)
+_add("sbuf", "int32", "WT", 1)
+_add("psum", "float32", "pA pB pK pD pY pS pI pJ", 512)
+
+SEMAPHORES = ["qv", "qa", "qt", "qp", "ls"] + ["d%d" % i for i in range(12)] + [
+    m + str(t) for m in ("aw", "ay", "am") for t in range(ST)]
+
+
+def rank_program(g, core, T, topo):
+    rank = T.rank_of(core)
+    if rank is None:
+        return
+    Q = {"v": g.vector, "a": g.scalar, "t": g.tensor, "p": g, "s": g.sync}
+    SEM = {"v": "qv", "a": "qa", "t": "qt", "p": "qp", "s": None}
+    cnt = {"qv": 0, "qa": 0, "qt": 0, "qp": 0, "ls": 0}
+    clk = {e: {} for e in Q}
+    acc = {n: [] for n in SCRATCH}
+    nd = [0]
+
+    def v(name, lo=0, hi=None, step=1, p0=0, p1=None):
+        sh = SCRATCH[name][1]
+        return (name, lo, sh[1] if hi is None else hi, step, p0, sh[0] if p1 is None else p1)
+
+    def ap(w):
+        if w[0] == "ind":
+            return ap(w[1]).indirect(ap(w[2]))
+        n, lo, hi, st, p0, p1 = w
+        if st == 1:
+            return T[n][p0:p1, lo:hi]
+        return T[n][p0:p1, lo:hi:st]
+
+    def ind(win, off):
+        return ("ind", win, off)
+
+    def meets(x, y):
+        if x[1] >= y[2] or y[1] >= x[2] or x[4] >= y[5] or y[4] >= x[5]:
+            return False
+        if x[3] == y[3] and x[3] > 1 and (x[1] - y[1]) % x[3]:
+            return False
+        return True
+
+    def covers(x, y):
+        return x[3] == 1 and x[1] <= y[1] and x[2] >= y[2] and x[4] <= y[4] and x[5] >= y[5]
+
+    def emit(eng, call, writes, reads, tok=None, inc=1, note=True):
+        ws, rs = [], []
+        for w in writes:
+            if w[0] == "ind":
+                ws.append(w[1]); rs.append(w[2])
+            else:
+                ws.append(w)
+        for w in reads:
+            if w[0] == "ind":
+                rs.append(w[1]); rs.append(w[2])
+            elif isinstance(w, tuple):
+                rs.append(w)
+        mysem = tok[0] if tok else SEM[eng]
+        need = {}
+        for lst, wr in ((rs, False), (ws, True)):
+            for w in lst:
+                psum = w[0][0] == "p"
+                for (tk, w2, wr2, ck2) in acc[w[0]]:
+                    same = tk[0] == mysem
+                    if psum and not same:
+                        hit = True
+                    elif same:
+                        hit = wr2 and not wr and meets(w, w2)
+                    else:
+                        hit = (wr or wr2) and meets(w, w2)
+                    if hit and clk[eng].get(tk[0], 0) < tk[1] and need.get(tk[0], (0,))[0] < tk[1]:
+                        need[tk[0]] = (tk[1], ck2)
+        ck = clk[eng]
+        for s in list(need):
+            val, c2 = need[s]
+            if any(s2 != s and need[s2][1].get(s, 0) >= val for s2 in need):
+                continue
+            Q[eng].wait_ge(T.sem[s], val)
+            for k2 in c2:
+                ck[k2] = max(ck.get(k2, 0), c2[k2])
+            ck[s] = max(ck.get(s, 0), val)
+        ins = call()
+        if not note:
+            return None
+        if tok is None:
+            cnt[mysem] += 1
+            tok = (mysem, cnt[mysem])
+        ins.then_inc(T.sem[tok[0]], inc)
+        snap = dict(ck)
+        snap[tok[0]] = tok[1]
+        record(tok, ws, rs, snap)
+        return tok
+
+    def record(tok, ws, rs, snap):
+        for w in rs:
+            old = acc[w[0]]
+            if w[0][0] == "p":
+                old = [x for x in old if x[0][0] == tok[0]]
+            acc[w[0]] = [x for x in old if not (x[0][0] == tok[0] and not x[2] and covers(w, x[1]))] + [(tok, w, False, snap)]
+        for w in ws:
+            old = acc[w[0]]
+            if w[0][0] == "p":
+                old = [x for x in old if x[0][0] == tok[0]]
+            acc[w[0]] = [x for x in old if not covers(w, x[1])] + [(tok, w, True, snap)]
+
+    def sc(x):
+        return ap(x) if isinstance(x, tuple) else x
+
+    def tc(o, i):
+        emit("v", lambda: g.vector.tensor_copy(ap(o), ap(i)), [o], [i])
+
+    def tt(o, x, y, op):
+        emit("v", lambda: g.vector.tensor_tensor(ap(o), ap(x), ap(y), op), [o], [x, y])
+
+    def ts(o, x, s1, op0, s2=None, op1=None):
+        r = [x] + [s for s in (s1, s2) if isinstance(s, tuple)]
+        if op1 is None:
+            emit("v", lambda: g.vector.tensor_scalar(ap(o), ap(x), sc(s1), None, op0), [o], r)
+        else:
+            emit("v", lambda: g.vector.tensor_scalar(ap(o), ap(x), sc(s1), sc(s2), op0, op1), [o], r)
+
+    def tr(o, x, op, ab=False):
+        emit("v", lambda: g.vector.tensor_reduce(ap(o), ap(x), AxisListType.X, op, apply_absolute_value=ab), [o], [x])
+
+    def ms(o, c):
+        emit("v", lambda: g.vector.memset(ap(o), c), [o], [])
+
+    def tp(o, x):
+        emit("v", lambda: g.vector.transpose(ap(o), ap(x)), [o], [x])
+
+    def act(o, x, f, bias=None, scale=1.0):
+        r = [x] + [s for s in (bias, scale) if isinstance(s, tuple)]
+        if bias is None:
+            emit("a", lambda: g.scalar.activation(ap(o), ap(x), f, scale=sc(scale)), [o], r)
+        else:
+            emit("a", lambda: g.scalar.activation(ap(o), ap(x), f, bias=sc(bias), scale=sc(scale)), [o], r)
+
+    def mm(o, l, r, start, stop):
+        emit("t", lambda: g.tensor.matmul(ap(o), ap(l), ap(r), start, stop), [o], [l, r])
+
+    def iota(o, pat, base, cm):
+        if SCRATCH[o[0]][2] == "int32":
+            emit("p", lambda: g.iota(ap(o), pat, base, cm), [o], [])
+        else:
+            emit("p", lambda: g.iota(ap(o), pat, base, cm, allow_small_or_imprecise_dtypes=True), [o], [])
+
+    def dma(eng, out, in_, writes, reads):
+        s = "d%d" % nd[0]
+        nd[0] += 1
+        emit(eng, lambda: Q[eng].dma_start(out, in_), writes, reads, tok=(s, 16), inc=16)
+        return s
+
+    scol = {}
+    jcol = {}
+
+    def S(nm, b=None):
+        if nm not in scol:
+            scol[nm] = 8 * len(scol)
+        c = scol[nm]
+        return v("SM", c, c + 8) if b is None else v("SM", c + b, c + b + 1)
+
+    def J(nm):
+        if nm not in jcol:
+            jcol[nm] = 8 * len(jcol)
+        c = jcol[nm]
+        return v("SI", c, c + 8)
+
+    def send(src, dst, width, sem, to):
+        rid, pid, _e = topo.addr(to)
+        m = topo.mask(core, to)
+        o, i = v(dst, 0, width), v(src, 0, width)
+        emit("p", lambda: g.remote_dma(ap(o), ap(i), T.sem[sem], T.sem.ls, pid, rid, m), [], [i], note=False)
+        cnt["ls"] += len(topo.engines(core, to))
+
+    dma("s", ap(v("VR")), T.vl[:], [v("VR")], [])
+    dma("a", ap(v("CR")), T.cl[:], [v("CR")], [])
+    dma("s", ap(v("X", 0, 2048)), T.xc[:, 0:2048], [v("X", 0, 2048)], [])
+    dma("a", ap(v("X", 2048, 4096)), T.xc[:, 2048:4096], [v("X", 2048, 4096)], [])
+    dma("s", ap(v("NR")), T.ln[:], [v("NR")], [])
+    dma("s", ap(v("THR8")), T.th[:], [v("THR8")], [])
+    dma("s", ap(v("WT")), T.wt[:], [v("WT")], [])
+
+    pi = v("SI", 232, 233)
+    pg = v("SI", 233, 234)
+    pa = v("SI", 234, 235)
+    pp = v("SI", 235, 236)
+    iota(pi, [[1, 1]], 0, 1)
+    iota(v("ROWI"), [[1, 143]], -15, 0)
+    iota(v("CIO"), [[1, 128]], 0, 0)
+    iota(S("BA"), [[16, 8]], 8064, 0)
+    iota(S("B8"), [[1, 8]], 0, 0)
+    iota(v("R0", 0, 256), [[1, 32], [0, 8]], 0, 0)
+    iota(v("R0", 256, 288), [[0, 4], [0, 8]], 64, 0)
+    iota(v("QT"), [[-128, 36], [0, 8]], 8064, 0)
+    iota(v("POS"), [[128, 36], [16, 8]], 0, 0)
+    iota(v("PP"), [[1, 36], [0, 8]], 0, 0)
+    ts(pg, pi, 4, A.arith_shift_right)
+    ts(pa, pi, 15, A.bitwise_and)
+    ts(pp, pi, 4, A.arith_shift_right, 1, A.bitwise_and)
+    pf, pgf, pg16, paf, od, ev, pa8 = [S("cols", b) for b in range(7)]
+    tc(od, pp)
+    ts(ev, pp, -1.0, A.mult, 1.0, A.add)
+    ts(pg16, pg, 16.0, A.mult)
+    tc(pf, pi)
+    tc(pgf, pg)
+    tc(paf, pa)
+    ts(pa8, pa, 8.0, A.mult)
+    ts(v("ID"), v("ROWI", 15, 143), pf, A.is_equal)
+    ts(v("IDM"), v("ROWI", 15, 143), pf, A.is_equal, float(-BIG), A.mult)
+    for nm, wv in (("WB1", 1.0), ("WBK", 16384.0), ("WB4", 4.0), ("WBM", -2.0)):
+        ts(v(nm), v("ROWI"), pg16, A.is_equal, wv, A.mult)
+    for t in range(ST):
+        ms(v("W%d" % t, 256 + 8 * t, 264 + 8 * t), -BIG)
+        if t:
+            ms(v("R%d" % t, 256 + 8 * t, 264 + 8 * t), 64.0)
+    ms(v("X", 4096, NX), 0.0)
+    ms(v("ZERO"), 0.0)
+    ms(v("ONES"), 1.0)
+
+    def turn(raw, w0, w1):
+        for b in range(8):
+            tp(v("TA", b, 256, 8), v("RT", b, 256, 8))
+            tp(v("TB", b, 256, 8), v("RU", b, 256, 8))
+        ts(v("TC", 0, 128), v("TA", 0, 128), ev, A.mult)
+        ts(v("TC", 128, 256), v("TB", 0, 128), ev, A.mult)
+        ts(v("TE", 0, 128), v("TB", 128, 256), od, A.mult)
+        ts(v("TE", 128, 256), v("TA", 128, 256), od, A.mult)
+        tt(w0, v("TC", 0, 128), v("TE", 0, 128), A.add)
+        tt(w1, v("TC", 128, 256), v("TE", 128, 256), A.add)
+
+    ts(v("OUT"), v("VR"), 4096.0, A.mult, float(-BIG), A.add)
+    tt(v("RT", 0, 128), v("OUT", 0, 256, 2), v("CR", 0, 256, 2), A.add)
+    tt(v("RT", 128, 256), v("OUT", 1, 256, 2), v("CR", 1, 256, 2), A.add)
+    tc(v("RU", 0, 128), v("RT", 128, 256))
+    tc(v("RU", 128, 256), v("RT", 0, 128))
+    turn(None, v("W0", 0, 128), v("W0", 128, 256))
+
+    def lists(t):
+        P = 32 + t
+        W = "W%d" % t
+        for r0, r1 in ((0, 9), (9, P)):
+            ts(v("VI", r0 * 8, r1 * 8), v(W, r0 * 8, r1 * 8), 12, A.arith_shift_right, 4095, A.bitwise_and)
+            tc(v("VL", r0 * 8, r1 * 8), v("VI", r0 * 8, r1 * 8))
+        ts(v("CI", 0, P * 8 - 16), v(W, 0, P * 8 - 16), 4095, A.bitwise_and)
+        tc(v("CL", 0, P * 8 - 16), v("CI", 0, P * 8 - 16))
+
+    def late_constants():
+        ts(S("wt", 0), v("WT"), 1.0, A.mult)
+        ts(v("WBW"), v("WB1"), S("wt", 0), A.mult)
+        ts(v("CIO"), v("CIO"), 4, A.arith_shift_right)
+        ts(v("BLK"), v("CIO"), pgf, A.is_equal)
+        ts(v("DG"), v("ROWI", 15, 31), paf, A.is_equal)
+        ts(v("POS"), v("POS"), paf, A.add)
+        ts(S("BA"), S("BA"), paf, A.add)
+        ts(S("II"), S("B8"), pa8, A.add)
+        ts(S("DUMP"), S("II"), 4096.0, A.add)
+        ts(S("KD"), S("DUMP"), 128.0, A.mult)
+        tt(S("KD"), S("KD"), S("II"), A.add)
+        ts(S("THR"), S("II"), -1.0, A.add, 0.5, A.mult)
+        ts(S("HC"), S("II"), 1.0, A.add, 0.5, A.mult)
+        ts(S("HI"), S("II"), 0.5, A.mult)
+        ts(v("IDN"), v("ID"), -1.0, A.mult)
+        ts(v("GB", 0, 128, 1, 0, 8), v("CIO", 0, 128, 1, 0, 8), v("SM", pf[1], pf[2], 1, 0, 8), A.is_equal)
+        thf = v("SM", scol["wt"] + 1, scol["wt"] + 2, 1, 0, 8)
+        tc(thf, v("THR8"))
+        mm(v("pS", 0, 1), v("GB", 0, 128, 1, 0, 8), thf, True, True)
+        tc(S("th", 0), v("pS", 0, 1))
+        tc(S("lim", 0), S("th", 0))
+
+    def dedupe(nm, t2, off):
+        kb, nc = S("kb"), S("nc")
+        ts(kb, t2, 128.0, A.mult)
+        tt(kb, kb, S("KD"), A.add)
+        for b in range(8):
+            act(v("EX", b * 16, b * 16 + 16), v("DG"), AF.Copy, scale=S("kb", b))
+        mm(v("pI", 0, 128), v("BLK"), v("EX"), True, True)
+        tt(nc, S("HC"), kb, A.subtract)
+
+    def dedupe1():
+        for b in range(8):
+            act(v("AA", b * 128, b * 128 + 128), v("pI", 0, 128), AF.Identity, bias=S("nc", b))
+
+    def dedupe2(t2, off):
+        for b in range(8):
+            tr(S("mn", b), v("AA", b * 128, b * 128 + 128), A.min, True)
+        tt(S("nd"), S("mn"), S("THR"), A.is_gt)
+        tt(S("t3"), t2, S("nd"), A.mult)
+        tt(S("t4"), S("t3"), S("DUMP"), A.add)
+        tc(v(off), S("t4"))
+
+    xwin = v("X")
+
+    def step(t):
+        P = 32 + t
+        P1, G = P + 1, P - 2
+        n8, m8, G8 = P * 8, P1 * 8, G * 8
+        W, R, Wn, Rn = "W%d" % t, "R%d" % t, "W%d" % (t + 1), "R%d" % (t + 1)
+        YR, M, LW, LY, LM = ["%s%d" % (k, t) for k in ("YR", "M", "LW", "LY", "LM")]
+        n, nn, V0, V0n, TH = S("n%d" % t), S("n%d" % (t + 1)), S("V0%d" % t), S("V0%d" % (t + 1)), S("lim", t)
+        d = 1 + t % 5
+        to, fr = T.cores[(rank + d) % N], T.cores[(rank - d) % N]
+        ne = len(topo.engines(fr, core))
+        for buf, sem, wd in ((LW, "aw", m8), (LY, "ay", 128 + m8), (LM, "am", 24)):
+            record((sem + str(t), ne), [v(buf, 0, wd)], [], {})
+
+        gc = [(0, 8), (8, 17), (17, 26), (26, G)]
+        vc = [(0, 9), (9, 18), (18, 27), (27, P)]
+
+        def gv(c):
+            r0, r1 = vc[c]
+            act(v("XV", r0 * 128, r1 * 128), ind(v("X", 0, 4096), v("VL", r0 * 8, r1 * 8)), AF.Copy, scale=0.5)
+
+        def hs(c):
+            r0, r1 = gc[c]
+            return [(r, min(r + 4, r1)) for r in range(r0, r1, 4)]
+
+        hb = ("pA", "pB", "pJ")
+
+        def idp(c):
+            for k, (r0, r1) in enumerate(hs(c)):
+                mm(v(hb[k], 0, (r1 - r0) * 128), v("ID"), v("XV", r0 * 128, r1 * 128), True, True)
+
+        def hh(c):
+            for k, (r0, r1) in enumerate(hs(c)):
+                tt(v("H", r0 * 128, r1 * 128), v("XV", r0 * 128 + 128, r1 * 128 + 128), v(hb[k], 0, (r1 - r0) * 128), A.add)
+
+        def dd(c):
+            r0, r1 = gc[c]
+            tt(v("D", r0 * 128, r1 * 128), ind(v("X", 0, 4096), v("CL", r0 * 8, r1 * 8)), v("H", r0 * 128, r1 * 128), A.subtract)
+
+        def aba(c):
+            r0, r1 = gc[c]
+            act(v("AB", r0 * 128, r1 * 128), v("D", r0 * 128, r1 * 128), AF.Abs)
+
+        def sums(bank, wb, buf, r0, r1, last):
+            for a in range(16):
+                mm(v(bank, r0 * 8, r1 * 8), v(wb, 15 - a, 143 - a), v(buf, r0 * 128 + a, r1 * 128, 16), False, last and a == 15)
+
+        gv(0)
+        if t == 0:
+            tc(n, v("NR"))
+        ts(S("L"), n, 4.0, A.is_ge)
+        tt(S("nL"), n, S("L"), A.mult)
+        ts(S("nm3"), n, -3.0, A.add)
+        if t == 0:
+            tc(V0, v("VI", 0, 8))
+        tt(v("DUPM", 0, G8), v(R, 0, G8), v(R, 8, G8 + 8), A.is_equal)
+        for b in range(8):
+            ts(v("INV", b, G8, 8), v(R, b, G8, 8), S("nm3", b), A.is_gt)
+        mm(v("pK", 0, G8), v("ID"), v("QT", 0, G8), True, False)
+        mm(v("pK", 0, G8), v("ID"), v(R, 0, G8), False, False)
+        mm(v("pD", 0, n8), v("ID"), v("ZERO", 0, n8), True, False)
+        gv(1)
+        idp(0)
+        gv(2)
+        hh(0)
+        dd(0)
+        idp(1)
+        sums("pD", "WBM", "XV", 0, 9, False)
+        hh(1)
+        idp(2)
+        sums("pD", "WBM", "XV", 9, 18, False)
+        aba(0)
+        sums("pK", "WBK", "AB", 0, 8, False)
+        gv(3)
+        dd(1)
+        hh(2)
+        idp(3)
+        sums("pD", "WBM", "XV", 18, 27, False)
+        aba(1)
+        sums("pK", "WBK", "AB", 8, 17, False)
+        dd(2)
+        hh(3)
+        sums("pD", "WBM", "XV", 27, P, False)
+        aba(2)
+        sums("pK", "WBK", "AB", 17, 26, False)
+        dd(3)
+        aba(3)
+        tt(v("MK", 0, G8), v("INV", 0, G8), v("DUPM", 0, G8), A.max)
+        mm(v("pK", 0, G8), v("IDM"), v("MK", 0, G8), False, False)
+        sums("pK", "WBK", "AB", gc[3][0], G, True)
+        tt(v("DW", 8, m8), v(W, 0, n8), v(W, 8, m8), A.subtract)
+        if t:
+            cj = v("SI", 236, 237)
+            tc(cj, v("pS", 400, 401))
+            ts(cj, cj, 31, A.bitwise_and)
+            tt(TH, S("th", 0), cj, A.add)
+        ts(v("Z0", 0, G8), v("VI", 0, G8), 4096.0, A.mult, float(-BIG), A.add)
+        tt(v("Z", 0, G8), v("Z0", 0, G8), v("VI", 8, G8 + 8), A.add)
+        if t == 0:
+            late_constants()
+
+        for b in range(8):
+            tr(S("mx", b), v("pK", b, G8, 8), A.max)
+        tc(J("mx"), S("mx"))
+        ts(J("q"), J("mx"), 8064, A.bitwise_and)
+        tt(S("jk"), S("BA"), J("q"), A.subtract)
+        tc(v("JL"), S("jk"))
+        tc(v("DK"), ind(v("D", 0, G * 128), v("JL")))
+        tt(v("TK"), ind(v("H", 0, G * 128), v("JL")), v("DK"), A.subtract)
+        Y = v(YR, 0, 128)
+        ts(Y, v("TK"), 0.0, A.max, 63.0, A.min)
+        for k in range(2):
+            ts(v("pY", k * 128, k * 128 + 128), Y, 0.5, A.mult)
+        ts(J("k"), J("mx"), 127, A.bitwise_and)
+        tc(S("k"), J("k"))
+        act(S("nk"), S("k"), AF.Copy, bias=-1.0, scale=-1.0)
+        act(S("k15"), S("k"), AF.Copy, bias=1.5)
+        act(S("bO"), S("mx"), AF.Copy, bias=0.5, scale=-1.0 / 128)
+        act(S("jb"), S("jk"), AF.Copy, bias=-0.5, scale=-1.0)
+        act(S("jb1"), S("jk"), AF.Copy, bias=-128.0, scale=-1.0)
+        for b in range(8):
+            act(v(YR, 128 + b, 128 + m8, 8), v(R, b, m8, 8), AF.Relu, bias=S("nk", b))
+        send(W, LW, m8, "aw%d" % t, to)
+        send(YR, LY, 128 + m8, "ay%d" % t, to)
+        for b in range(8):
+            act(v("pA", b, n8, 8), v(R, b, n8, 8), AF.Relu, bias=S("k15", b), scale=-1.0)
+        for b in range(8):
+            act(v("RQ", b, n8, 8), v(R, b, n8, 8), AF.Relu, bias=S("nL", b), scale=-1.0)
+        for b in range(8):
+            act(v("pB", b, G8, 8), v("pK", b, G8, 8), AF.Sign, bias=S("bO", b), scale=1.0 / 128)
+
+        for a in range(16):
+            mm(v("pS", 304, 312), v("WB1", 15 - a, 143 - a), v(YR, a, 128, 16), a == 0, a == 15)
+        dc = [(2, 8), (8, 16), (16, 24), (24, P)]
+        for c, (r0, r1) in enumerate(dc):
+            for r in range(r0, r1, 2):
+                e = min(r + 2, r1)
+                tt(v("AB", r * 128, e * 128), v("XV", r * 128, e * 128), v("pY", 0, (e - r) * 128), A.max)
+            sums("pD", "WB4", "AB", r0, r1, c == 3)
+            if c == 1:
+                ts(S("lm"), v("pS", 304, 312), TH, A.add)
+                for b in range(8):
+                    act(v("LX", b, n8, 8), v("pA", b, n8, 8), AF.Identity, bias=S("lm", b), scale=-8192.0)
+                for b in range(8):
+                    act(v("SP", b, m8, 8), v("POS", b, m8, 8), AF.Sign, bias=S("jb", b))
+                for b in range(8):
+                    act(v("OA", b, m8, 8), v("POS", b, m8, 8), AF.Abs, bias=S("jb1", b))
+                act(v("OA", 0, m8), v("OA", 0, m8), AF.Relu, bias=1.0, scale=-1.0)
+        for a in range(16):
+            mm(v("pI", 0, 8), v("WBW", 15 - a, 143 - a), v(YR, a, 128, 16), a == 0, a == 15)
+        mm(v("pY", 8, m8), v("ID"), v("ONES", 8, m8), True, False)
+        mm(v("pY", 8, m8), v("ID"), v(R, 0, n8), False, False)
+        mm(v("pY", 8, m8), v("IDN"), v(R, 8, m8), False, True)
+        tt(S("nk1"), n, S("nk"), A.add)
+        tt(v("PZ", 0, G8), v("pB", 0, G8), v("Z", 0, G8), A.mult)
+        for b in range(8):
+            tr(S("z", b), v("PZ", b, G8, 8), A.min)
+        tc(J("z"), S("z"))
+        ts(J("vk"), J("z"), 12, A.arith_shift_right, 4095, A.bitwise_and)
+        ts(J("vk1"), J("z"), 4095, A.bitwise_and)
+        tc(v(M, 8, 16), J("vk1"))
+        tc(v(M, 16, 24), S("L"))
+        tt(v("pA", 0, n8), v("pD", 0, n8), v("LX", 0, n8), A.is_le)
+        tt(v("PZ", 0, n8), v("pA", 0, n8), v("RQ", 0, n8), A.mult)
+        for b in range(8):
+            tr(S("vm", b), v("PZ", b, n8, 8), A.max)
+        ts(S("cl"), S("vm"), 0.0, A.is_gt)
+        ts(S("vp"), S("vm"), 0.0, A.max)
+        tt(S("sz0"), S("cl"), S("nk1"), A.mult)
+        tt(v(M, 0, 8), S("sz0"), S("vp"), A.subtract)
+        sz = v(M, 0, 8)
+        send(M, LM, 24, "am%d" % t, to)
+        tt(S("gr"), S("L"), S("cl"), A.subtract)
+        for b in range(8):
+            act(v("GG", b, m8, 8), v("SP", b, m8, 8), AF.Relu, scale=S("gr", b))
+
+        tc(J("u"), v("pI", 0, 8))
+        ts(J("u2"), J("u"), 4095, A.bitwise_and)
+        tt(J("uu"), J("u2"), J("u2"), A.mult)
+        ts(J("v37"), J("vk"), 37.0, A.mult)
+        ts(J("us"), J("uu"), 5, A.arith_shift_right)
+        tt(J("h0"), J("us"), J("v37"), A.add)
+        ts(J("h"), J("h0"), 4095, A.bitwise_and)
+        tt(S("hd"), J("h"), S("DUMP"), A.subtract)
+        tt(S("t2g"), S("hd"), S("gr"), A.mult)
+        dedupe("g", S("t2g"), "OL")
+        tt(v("pA", 8, m8), v("GG", 8, m8), v("pY", 8, m8), A.mult)
+        tt(v("pB", 8, m8), v("GG", 8, m8), v("DW", 8, m8), A.mult)
+        tt(v("RA", 8, m8), v(R, 8, m8), v("pA", 8, m8), A.add)
+        tt(v("WA", 8, m8), v(W, 8, m8), v("pB", 8, m8), A.add)
+        tc(v("RA", 0, 8), v(R, 0, 8))
+        tc(v("WA", 0, 8), v(W, 0, 8))
+        tt(S("ks"), S("k"), sz, A.add)
+        tt(S("zl"), S("z"), S("L"), A.mult)
+        ts(S("wn0"), J("h"), 4096.0, A.mult, float(-BIG), A.add)
+        tt(S("wn1"), S("wn0"), J("vk"), A.add)
+        tt(S("wn"), S("wn1"), S("gr"), A.mult)
+        for b in range(8):
+            ts(v("pA", b, m8, 8), v("RA", b, m8, 8), S("k", b), A.max, S("ks", b), A.min)
+        tt(v("E", 0, m8), v("RA", 0, m8), v("pA", 0, m8), A.subtract)
+        act(v("YX", 0, 8), S("cl"), AF.Copy)
+        act(S("rest"), S("L"), AF.Copy, bias=1.0, scale=-1.0)
+        for b in range(8):
+            act(v("AA", b * 128, b * 128 + 128), v("pI", 0, 128), AF.Abs, bias=S("nc", b))
+        for b in range(8):
+            x = v("AA", b * 128, b * 128 + 128)
+            o = v("AB", b * 128, b * 128 + 128)
+            emit("a", lambda: g.scalar.activation(ap(o), ap(x), AF.Relu, bias=ap(S("HI", b)), scale=-1.0, accum_out=ap(S("hit", b))),
+                 [o, S("hit", b)], [x, S("HI", b)])
+        tt(S("ng"), n, S("gr"), A.add)
+        ts(S("ng"), S("ng"), 32.0, A.min)
+        tt(S("n2"), S("ng"), sz, A.subtract)
+        ts(S("nd"), S("hit"), 0.0, A.is_equal)
+        tt(S("t3"), S("t2g"), S("nd"), A.mult)
+        tt(S("t4"), S("t3"), S("DUMP"), A.add)
+        tc(v("OL"), S("t4"))
+        tc(ind(xwin, v("OL")), Y)
+        act(v("RQ", 0, m8), v("E", 0, m8), AF.Abs)
+        act(v("RQ", 0, m8), v("RQ", 0, m8), AF.Relu, bias=1.0, scale=-1.0)
+        for b in range(8):
+            act(v("T1", b, m8, 8), v("RQ", b, m8, 8), AF.Copy, scale=S("zl", b))
+        for b in range(8):
+            act(v("pD", b, m8, 8), v("OA", b, m8, 8), AF.Copy, scale=S("wn", b))
+        for b in range(8):
+            act(v("RX", b, m8, 8), v("E", b, m8, 8), AF.Identity, bias=S("k", b))
+        mm(v("pS", 0, m8), v("ID"), v(LY, 128, 128 + m8), True, False)
+        mm(v("pS", 0, m8), v("IDN"), v(R, 0, m8), False, True)
+        if t < ST - 1:
+            for b in range(8):
+                mm(v("pS", 400, 401), v("ONES", 0, 128), v("YX", b, b + 1), b == 0, b == 7)
+
+        tt(S("tk0"), v(LM, 0, 8), S("n2"), A.is_gt)
+        tt(S("tk"), S("tk0"), S("rest"), A.mult)
+        tt(S("dn"), v(LM, 0, 8), S("n2"), A.subtract)
+        tt(S("dn"), S("dn"), S("tk"), A.mult)
+        tt(nn, S("n2"), S("dn"), A.add)
+        tt(S("dv"), v(LM, 8, 16), V0, A.subtract)
+        tt(S("dv"), S("dv"), S("tk"), A.mult)
+        tt(V0n, V0, S("dv"), A.add)
+        ts(S("has0"), nn, 1.0, A.is_ge)
+        tt(S("has"), S("has0"), v(LM, 16, 24), A.mult)
+        tt(S("vd"), V0n, S("DUMP"), A.subtract)
+        tt(S("t2b"), S("vd"), S("has"), A.mult)
+        dedupe("b", S("t2b"), "OB")
+        tt(v("TM", 0, m8), v("T1", 0, m8), v("pD", 0, m8), A.add)
+        for b in range(8):
+            ts(v("pK", b, m8, 8), v(LW, b, m8, 8), S("tk", b), A.mult)
+        tt(v("TM", 0, m8), v("TM", 0, m8), v("pK", 0, m8), A.add)
+        ts(v("pA", 0, m8), v("TM", 0, m8), 0.0, A.is_equal)
+        tt(v("pB", 0, m8), v("WA", 0, m8), v("pA", 0, m8), A.mult)
+        tt(v(Wn, 0, m8), v("TM", 0, m8), v("pB", 0, m8), A.add)
+        dedupe1()
+        for b in range(8):
+            act(v("pJ", b, m8, 8), v("pS", b, m8, 8), AF.Copy, scale=S("tk", b))
+        dedupe2(S("t2b"), "OB")
+        tt(v("BS"), ind(xwin, v("OB")), v(LY, 0, 128), A.add)
+        ts(v("BO"), v("BS"), 0.5, A.mult, -0.25, A.add)
+        tc(ind(xwin, v("OB")), v("BO"))
+        if t < ST - 1:
+            lists(t + 1)
+        tt(v(Rn, 0, m8), v("RX", 0, m8), v("pJ", 0, m8), A.add)
+
+    lists(0)
+    for t in range(ST):
+        step(t)
+
+    so = [dma("s", T.yx[:, 0:2048], ap(v("X", 0, 2048)), [], [v("X", 0, 2048)]),
+          dma("a", T.yx[:, 2048:4096], ap(v("X", 2048, 4096)), [], [v("X", 2048, 4096)]),
+          dma("s", T.yn[:], ap(S("n4")), [], [S("n4")])]
+    n = S("n4")
+    ms(v("T1", 280, 288), 1.0)
+    tt(v("T1", 0, 280), v("R4", 0, 280), v("R4", 8, 288), A.not_equal)
+    for b in range(8):
+        ts(v("pA", b, 288, 8), v("R4", b, 288, 8), S("n4", b), A.is_lt)
+    tt(v("E"), v("T1"), v("pA", 0, 288), A.mult)
+    ts(v("U"), v("W4"), float(BIG), A.add)
+    tt(v("U"), v("U"), v("E"), A.mult)
+    tt(v("CV"), v("PP"), v("R4"), A.subtract)
+    tt(v("DLT"), v("CV"), v("E"), A.mult)
+    for i in range(6):
+        lo = 8 << i
+        w = 288 - lo
+        ts(v("BIT", lo, 288), v("DLT", lo, 288), i, A.arith_shift_right, 1, A.bitwise_and)
+        tc(v("pA", lo, 288), v("BIT", lo, 288))
+        tt(v("pB", lo, 288), v("U", lo, 288), v("pA", lo, 288), A.mult)
+        tt(v("pK", lo, 288), v("DLT", lo, 288), v("pA", lo, 288), A.mult)
+        tt(v("U", lo, 288), v("U", lo, 288), v("pB", lo, 288), A.subtract)
+        tt(v("DLT", lo, 288), v("DLT", lo, 288), v("pK", lo, 288), A.subtract)
+        tt(v("U", 0, w), v("U", 0, w), v("pB", lo, 288), A.add)
+        tt(v("DLT", 0, w), v("DLT", 0, w), v("pK", lo, 288), A.add)
+    tc(v("RT"), v("U", 0, 256))
+    tc(v("RU", 0, 128), v("U", 128, 256))
+    tc(v("RU", 128, 256), v("U", 0, 128))
+    turn(None, v("OI", 0, 256, 2), v("OI", 1, 256, 2))
+    ts(v("VI", 0, 256), v("OI"), 12, A.arith_shift_right)
+    tc(v("OV"), v("VI", 0, 256))
+    so.append(dma("s", T.yv[:], ap(v("OV")), [], [v("OV")]))
+    ts(v("CI", 0, 256), v("OI"), 4095, A.bitwise_and)
+    tc(v("OC"), v("CI", 0, 256))
+    so.append(dma("a", T.yc[:], ap(v("OC")), [], [v("OC")]))
+    for s in so:
+        g.sync.wait_ge(T.sem[s], 16)
+    for s in ("qv", "qa", "qt", "qp"):
+        g.sync.wait_ge(T.sem[s], cnt[s])
+    g.wait_ge(T.sem.ls, cnt["ls"])

@@ -20,8 +20,8 @@ def _add(where, dtype, names, cols, rows=128):
 _add("sbuf", "bfloat16", "X", NX)
 _add("sbuf", "bfloat16", "XV H D AB", 4480)
 _add("sbuf", "int32", "W0 W1 W2 W3 W4 LW0 LW1 LW2 LW3 VI CI DLT BIT", 288)
-_add("sbuf", "bfloat16", "R0 R1 R2 R3 R4 QT ZERO ONES DUPM INV MK RB", 288)
-_add("sbuf", "float32", "POS Z Z0 DW RQ LX OA SP GG PZ WA RA CV E T1 TM RX PP U TDB", 288)
+_add("sbuf", "bfloat16", "R0 R1 R2 R3 R4 QT ZERO ONES INV MK PP", 288)
+_add("sbuf", "float32", "POS Z Z0 DW RQ LX OA SP GG PZ WA RA A2 E T1 TM RX U", 288)
 _add("sbuf", "uint16", "VL CL", 288)
 _add("sbuf", "uint16", "JL OL OB", 8)
 _add("sbuf", "bfloat16", "YR0 YR1 YR2 YR3 LY0 LY1 LY2 LY3", 416)
@@ -30,8 +30,8 @@ _add("sbuf", "float32", "SM", 720)
 _add("sbuf", "int32", "SI", 240)
 _add("sbuf", "float32", "ROWI", 143)
 _add("sbuf", "bfloat16", "WB1 WBK WB4 WBM WBW", 143)
-_add("sbuf", "bfloat16", "ID IDM IDN DK TK BI YX", 128)
-_add("sbuf", "float32", "BLK GB EX", 128)
+_add("sbuf", "bfloat16", "ID IDM IDH IDN DK TK BI YX", 128)
+_add("sbuf", "float32", "BLK GB EX EXC", 128)
 _add("sbuf", "int32", "CIO BO", 128)
 _add("sbuf", "float32", "BS", 128)
 _add("sbuf", "float32", "DG", 16)
@@ -216,11 +216,11 @@ def rank_program(g, core, T, topo):
 
     dma("s", ap(v("VR")), T.vl[:], [v("VR")], [])
     dma("a", ap(v("CR")), T.cl[:], [v("CR")], [])
-    dma("s", ap(v("X", 0, 2048)), T.xc[:, 0:2048], [v("X", 0, 2048)], [])
     dma("a", ap(v("X", 2048, 4096)), T.xc[:, 2048:4096], [v("X", 2048, 4096)], [])
+    dma("s", ap(v("X", 0, 2048)), T.xc[:, 0:2048], [v("X", 0, 2048)], [])
     dma("s", ap(v("NR")), T.ln[:], [v("NR")], [])
-    dma("s", ap(v("THR8")), T.th[:], [v("THR8")], [])
-    dma("s", ap(v("WT")), T.wt[:], [v("WT")], [])
+    dma("a", ap(v("THR8")), T.th[:], [v("THR8")], [])
+    dma("a", ap(v("WT")), T.wt[:], [v("WT")], [])
 
     pi = v("SI", 232, 233)
     pg = v("SI", 233, 234)
@@ -249,6 +249,8 @@ def rank_program(g, core, T, topo):
     ts(pa8, pa, 8.0, A.mult)
     ts(v("ID"), v("ROWI", 15, 143), pf, A.is_equal)
     ts(v("IDM"), v("ROWI", 15, 143), pf, A.is_equal, float(-BIG), A.mult)
+    ts(v("IDH"), v("ID"), float(-BIG // 2), A.mult)
+    ts(v("IDN"), v("ID"), -1.0, A.mult)
     for nm, wv in (("WB1", 1.0), ("WBK", 16384.0), ("WB4", 4.0), ("WBM", -2.0)):
         ts(v(nm), v("ROWI"), pg16, A.is_equal, wv, A.mult)
     for t in range(ST):
@@ -261,7 +263,7 @@ def rank_program(g, core, T, topo):
 
     def turn(raw, w0, w1):
         for b in range(8):
-            tp(v("TA", b, 256, 8), v("RT", b, 256, 8))
+            tp(v("TA", b, 256, 8), v(raw, b, 256, 8))
             tp(v("TB", b, 256, 8), v("RU", b, 256, 8))
         ts(v("TC", 0, 128), v("TA", 0, 128), ev, A.mult)
         ts(v("TC", 128, 256), v("TB", 0, 128), ev, A.mult)
@@ -275,7 +277,7 @@ def rank_program(g, core, T, topo):
     tt(v("RT", 128, 256), v("OUT", 1, 256, 2), v("CR", 1, 256, 2), A.add)
     tc(v("RU", 0, 128), v("RT", 128, 256))
     tc(v("RU", 128, 256), v("RT", 0, 128))
-    turn(None, v("W0", 0, 128), v("W0", 128, 256))
+    turn("RT", v("W0", 0, 128), v("W0", 128, 256))
 
     def lists(t):
         P = 32 + t
@@ -291,17 +293,14 @@ def rank_program(g, core, T, topo):
         ts(v("WBW"), v("WB1"), S("wt", 0), A.mult)
         ts(v("CIO"), v("CIO"), 4, A.arith_shift_right)
         ts(v("BLK"), v("CIO"), pgf, A.is_equal)
-        ts(v("DG"), v("ROWI", 15, 31), paf, A.is_equal)
+        ts(v("DG"), v("ROWI", 15, 31), paf, A.is_equal, 128.0, A.mult)
         ts(v("POS"), v("POS"), paf, A.add)
         ts(S("BA"), S("BA"), paf, A.add)
         ts(S("II"), S("B8"), pa8, A.add)
         ts(S("DUMP"), S("II"), 4096.0, A.add)
-        ts(S("KD"), S("DUMP"), 128.0, A.mult)
-        tt(S("KD"), S("KD"), S("II"), A.add)
-        ts(S("THR"), S("II"), -1.0, A.add, 0.5, A.mult)
-        ts(S("HC"), S("II"), 1.0, A.add, 0.5, A.mult)
-        ts(S("HI"), S("II"), 0.5, A.mult)
-        ts(v("IDN"), v("ID"), -1.0, A.mult)
+        ts(S("KF0"), S("II"), 1.0 / 128, A.mult)
+        tt(S("KF"), S("KF0"), S("DUMP"), A.add)
+        tt(S("V00"), v("VI", 0, 8), S("DUMP"), A.subtract)
         ts(v("GB", 0, 128, 1, 0, 8), v("CIO", 0, 128, 1, 0, 8), v("SM", pf[1], pf[2], 1, 0, 8), A.is_equal)
         thf = v("SM", scol["wt"] + 1, scol["wt"] + 2, 1, 0, 8)
         tc(thf, v("THR8"))
@@ -309,23 +308,49 @@ def rank_program(g, core, T, topo):
         tc(S("th", 0), v("pS", 0, 1))
         tc(S("lim", 0), S("th", 0))
 
-    def dedupe(nm, t2, off):
-        kb, nc = S("kb"), S("nc")
-        ts(kb, t2, 128.0, A.mult)
-        tt(kb, kb, S("KD"), A.add)
+    def scalar_constants():
+        act(S("THR"), S("II"), AF.Copy, bias=-0.5, scale=0.5)
+        act(S("HC"), S("II"), AF.Copy, bias=0.5, scale=0.5)
+        act(S("HI"), S("II"), AF.Copy, scale=0.5)
+        act(S("KD"), S("KF"), AF.Copy, scale=128.0)
         for b in range(8):
-            act(v("EX", b * 16, b * 16 + 16), v("DG"), AF.Copy, scale=S("kb", b))
-        mm(v("pI", 0, 128), v("BLK"), v("EX"), True, True)
-        tt(nc, S("HC"), kb, A.subtract)
+            act(v("EXC", b * 16, b * 16 + 16), v("DG"), AF.Copy, scale=S("KF", b))
+        tt(S("HK"), S("HC"), S("KD"), A.subtract)
 
-    def dedupe1():
+    def masks(t):
+        R, G8 = "R%d" % t, (30 + t) * 8
+        mm(v("pA", 0, G8), v("ID"), v(R, 8, G8 + 8), True, False)
+        mm(v("pA", 0, G8), v("IDN"), v(R, 0, G8), False, True)
+        act(S("b25"), S("n%d" % t), AF.Copy, bias=2.5, scale=-1.0)
         for b in range(8):
-            act(v("AA", b * 128, b * 128 + 128), v("pI", 0, 128), AF.Identity, bias=S("nc", b))
+            act(v("INV", b, G8, 8), v(R, b, G8, 8), AF.Sign, bias=S("b25", b))
+        act(v("MK", 0, G8), v("pA", 0, G8), AF.Relu, bias=1.0, scale=-1.0)
+
+    def dedupe(t2):
+        mm(v("pI", 0, 128), v("BLK"), v("EXC"), True, False)
+        for b in range(8):
+            act(v("EX", b * 16, b * 16 + 16), v("DG"), AF.Copy, scale=v("SM", t2[1] + b, t2[1] + b + 1))
+        mm(v("pI", 0, 128), v("BLK"), v("EX"), False, True)
+        ts(S("nc0"), t2, -128.0, A.mult)
+        tt(S("nc"), S("nc0"), S("HK"), A.add)
+
+    def far(b):
+        act(v("AA", b * 128, b * 128 + 128), v("pI", 0, 128), AF.Abs, bias=S("nc", b))
+
+    def hit(b):
+        x, o = v("AA", b * 128, b * 128 + 128), v("AB", b * 128, b * 128 + 128)
+        emit("a", lambda: g.scalar.activation(ap(o), ap(x), AF.Relu, bias=ap(S("HI", b)), scale=-1.0, accum_out=ap(S("hit", b))),
+             [o, S("hit", b)], [x, S("HI", b)])
+
+    def half(nm, k):
+        c = S(nm)[1]
+        return v("SM", c + 4 * k, c + 4 * k + 4)
 
     def dedupe2(t2, off):
-        for b in range(8):
-            tr(S("mn", b), v("AA", b * 128, b * 128 + 128), A.min, True)
-        tt(S("nd"), S("mn"), S("THR"), A.is_gt)
+        for b in range(4):
+            tr(S("mn", b), v("AA", b * 128, b * 128 + 128), A.min)
+        tt(half("nd", 0), half("mn", 0), half("THR", 0), A.is_gt)
+        ts(half("nd", 1), half("hit", 1), 0.0, A.is_equal)
         tt(S("t3"), t2, S("nd"), A.mult)
         tt(S("t4"), S("t3"), S("DUMP"), A.add)
         tc(v(off), S("t4"))
@@ -350,7 +375,8 @@ def rank_program(g, core, T, topo):
 
         def gv(c):
             r0, r1 = vc[c]
-            act(v("XV", r0 * 128, r1 * 128), ind(v("X", 0, 4096), v("VL", r0 * 8, r1 * 8)), AF.Copy, scale=0.5)
+            for r0, r1 in ([(0, 5), (5, r1)] if c == 0 else [(r0, r1)]):
+                act(v("XV", r0 * 128, r1 * 128), ind(v("X", 0, 4096), v("VL", r0 * 8, r1 * 8)), AF.Copy, scale=0.5)
 
         def hs(c):
             r0, r1 = gc[c]
@@ -380,20 +406,18 @@ def rank_program(g, core, T, topo):
 
         gv(0)
         if t == 0:
-            tc(n, v("NR"))
+            masks(0)
+            late_constants()
         ts(S("L"), n, 4.0, A.is_ge)
         tt(S("nL"), n, S("L"), A.mult)
-        ts(S("nm3"), n, -3.0, A.add)
-        if t == 0:
-            tc(V0, v("VI", 0, 8))
-        tt(v("DUPM", 0, G8), v(R, 0, G8), v(R, 8, G8 + 8), A.is_equal)
-        for b in range(8):
-            ts(v("INV", b, G8, 8), v(R, b, G8, 8), S("nm3", b), A.is_gt)
+        idp(0)
         mm(v("pK", 0, G8), v("ID"), v("QT", 0, G8), True, False)
         mm(v("pK", 0, G8), v("ID"), v(R, 0, G8), False, False)
+        mm(v("pK", 0, G8), v("IDH"), v("ONES", 0, G8), False, False)
+        mm(v("pK", 0, G8), v("IDH"), v("INV", 0, G8), False, False)
+        mm(v("pK", 0, G8), v("IDM"), v("MK", 0, G8), False, False)
         mm(v("pD", 0, n8), v("ID"), v("ZERO", 0, n8), True, False)
         gv(1)
-        idp(0)
         gv(2)
         hh(0)
         dd(0)
@@ -413,14 +437,12 @@ def rank_program(g, core, T, topo):
         sums("pK", "WBK", "AB", 8, 17, False)
         dd(2)
         hh(3)
-        sums("pD", "WBM", "XV", 27, P, False)
         aba(2)
         sums("pK", "WBK", "AB", 17, 26, False)
         dd(3)
         aba(3)
-        tt(v("MK", 0, G8), v("INV", 0, G8), v("DUPM", 0, G8), A.max)
-        mm(v("pK", 0, G8), v("IDM"), v("MK", 0, G8), False, False)
         sums("pK", "WBK", "AB", gc[3][0], G, True)
+        sums("pD", "WBM", "XV", 27, P, False)
         tt(v("DW", 8, m8), v(W, 0, n8), v(W, 8, m8), A.subtract)
         if t:
             cj = v("SI", 236, 237)
@@ -430,7 +452,7 @@ def rank_program(g, core, T, topo):
         ts(v("Z0", 0, G8), v("VI", 0, G8), 4096.0, A.mult, float(-BIG), A.add)
         tt(v("Z", 0, G8), v("Z0", 0, G8), v("VI", 8, G8 + 8), A.add)
         if t == 0:
-            late_constants()
+            scalar_constants()
 
         for b in range(8):
             tr(S("mx", b), v("pK", b, G8, 8), A.max)
@@ -448,6 +470,8 @@ def rank_program(g, core, T, topo):
         tc(S("k"), J("k"))
         act(S("nk"), S("k"), AF.Copy, bias=-1.0, scale=-1.0)
         act(S("k15"), S("k"), AF.Copy, bias=1.5)
+        act(S("kn"), S("k"), AF.Copy, scale=-1.0)
+        act(v(M, 16, 24), S("L"), AF.Copy)
         act(S("bO"), S("mx"), AF.Copy, bias=0.5, scale=-1.0 / 128)
         act(S("jb"), S("jk"), AF.Copy, bias=-0.5, scale=-1.0)
         act(S("jb1"), S("jk"), AF.Copy, bias=-128.0, scale=-1.0)
@@ -479,6 +503,8 @@ def rank_program(g, core, T, topo):
                 for b in range(8):
                     act(v("OA", b, m8, 8), v("POS", b, m8, 8), AF.Abs, bias=S("jb1", b))
                 act(v("OA", 0, m8), v("OA", 0, m8), AF.Relu, bias=1.0, scale=-1.0)
+                for b in range(8):
+                    act(v("A2", b, m8, 8), v(R, b, m8, 8), AF.Relu, bias=S("k", b), scale=-1.0)
         for a in range(16):
             mm(v("pI", 0, 8), v("WBW", 15 - a, 143 - a), v(YR, a, 128, 16), a == 0, a == 15)
         mm(v("pY", 8, m8), v("ID"), v("ONES", 8, m8), True, False)
@@ -491,8 +517,7 @@ def rank_program(g, core, T, topo):
         tc(J("z"), S("z"))
         ts(J("vk"), J("z"), 12, A.arith_shift_right, 4095, A.bitwise_and)
         ts(J("vk1"), J("z"), 4095, A.bitwise_and)
-        tc(v(M, 8, 16), J("vk1"))
-        tc(v(M, 16, 24), S("L"))
+        tt(v(M, 8, 16), J("vk1"), S("DUMP"), A.subtract)
         tt(v("pA", 0, n8), v("pD", 0, n8), v("LX", 0, n8), A.is_le)
         tt(v("PZ", 0, n8), v("pA", 0, n8), v("RQ", 0, n8), A.mult)
         for b in range(8):
@@ -516,115 +541,118 @@ def rank_program(g, core, T, topo):
         ts(J("h"), J("h0"), 4095, A.bitwise_and)
         tt(S("hd"), J("h"), S("DUMP"), A.subtract)
         tt(S("t2g"), S("hd"), S("gr"), A.mult)
-        dedupe("g", S("t2g"), "OL")
+        dedupe(S("t2g"))
+        ts(S("wn0"), J("h"), 4096.0, A.mult, float(-BIG), A.add)
+        tt(S("wn1"), S("wn0"), J("vk"), A.add)
+        tt(S("wn"), S("wn1"), S("gr"), A.mult)
+        for b in range(8):
+            act(v("pD", b, m8, 8), v("OA", b, m8, 8), AF.Copy, scale=S("wn", b))
         tt(v("pA", 8, m8), v("GG", 8, m8), v("pY", 8, m8), A.mult)
         tt(v("pB", 8, m8), v("GG", 8, m8), v("DW", 8, m8), A.mult)
         tt(v("RA", 8, m8), v(R, 8, m8), v("pA", 8, m8), A.add)
         tt(v("WA", 8, m8), v(W, 8, m8), v("pB", 8, m8), A.add)
         tc(v("RA", 0, 8), v(R, 0, 8))
         tc(v("WA", 0, 8), v(W, 0, 8))
-        tt(S("ks"), S("k"), sz, A.add)
+        tt(S("kns"), S("kn"), sz, A.subtract)
         tt(S("zl"), S("z"), S("L"), A.mult)
-        ts(S("wn0"), J("h"), 4096.0, A.mult, float(-BIG), A.add)
-        tt(S("wn1"), S("wn0"), J("vk"), A.add)
-        tt(S("wn"), S("wn1"), S("gr"), A.mult)
-        for b in range(8):
-            ts(v("pA", b, m8, 8), v("RA", b, m8, 8), S("k", b), A.max, S("ks", b), A.min)
-        tt(v("E", 0, m8), v("RA", 0, m8), v("pA", 0, m8), A.subtract)
         act(v("YX", 0, 8), S("cl"), AF.Copy)
         act(S("rest"), S("L"), AF.Copy, bias=1.0, scale=-1.0)
         for b in range(8):
-            act(v("AA", b * 128, b * 128 + 128), v("pI", 0, 128), AF.Abs, bias=S("nc", b))
+            far(b)
+        for b in range(4, 8):
+            hit(b)
         for b in range(8):
-            x = v("AA", b * 128, b * 128 + 128)
-            o = v("AB", b * 128, b * 128 + 128)
-            emit("a", lambda: g.scalar.activation(ap(o), ap(x), AF.Relu, bias=ap(S("HI", b)), scale=-1.0, accum_out=ap(S("hit", b))),
-                 [o, S("hit", b)], [x, S("HI", b)])
+            act(v("pA", b, m8, 8), v("RA", b, m8, 8), AF.Relu, bias=S("kns", b))
         tt(S("ng"), n, S("gr"), A.add)
         ts(S("ng"), S("ng"), 32.0, A.min)
         tt(S("n2"), S("ng"), sz, A.subtract)
-        ts(S("nd"), S("hit"), 0.0, A.is_equal)
-        tt(S("t3"), S("t2g"), S("nd"), A.mult)
-        tt(S("t4"), S("t3"), S("DUMP"), A.add)
-        tc(v("OL"), S("t4"))
+        dedupe2(S("t2g"), "OL")
         tc(ind(xwin, v("OL")), Y)
+        tt(v("E", 0, m8), v("pA", 0, m8), v("A2", 0, m8), A.subtract)
         act(v("RQ", 0, m8), v("E", 0, m8), AF.Abs)
         act(v("RQ", 0, m8), v("RQ", 0, m8), AF.Relu, bias=1.0, scale=-1.0)
-        for b in range(8):
-            act(v("T1", b, m8, 8), v("RQ", b, m8, 8), AF.Copy, scale=S("zl", b))
-        for b in range(8):
-            act(v("pD", b, m8, 8), v("OA", b, m8, 8), AF.Copy, scale=S("wn", b))
-        for b in range(8):
-            act(v("RX", b, m8, 8), v("E", b, m8, 8), AF.Identity, bias=S("k", b))
         mm(v("pS", 0, m8), v("ID"), v(LY, 128, 128 + m8), True, False)
         mm(v("pS", 0, m8), v("IDN"), v(R, 0, m8), False, True)
         if t < ST - 1:
             for b in range(8):
                 mm(v("pS", 400, 401), v("ONES", 0, 128), v("YX", b, b + 1), b == 0, b == 7)
 
-        tt(S("tk0"), v(LM, 0, 8), S("n2"), A.is_gt)
-        tt(S("tk"), S("tk0"), S("rest"), A.mult)
-        tt(S("dn"), v(LM, 0, 8), S("n2"), A.subtract)
-        tt(S("dn"), S("dn"), S("tk"), A.mult)
-        tt(nn, S("n2"), S("dn"), A.add)
+        tt(S("rc"), v(LM, 0, 8), S("rest"), A.mult)
         tt(S("dv"), v(LM, 8, 16), V0, A.subtract)
-        tt(S("dv"), S("dv"), S("tk"), A.mult)
-        tt(V0n, V0, S("dv"), A.add)
-        ts(S("has0"), nn, 1.0, A.is_ge)
-        tt(S("has"), S("has0"), v(LM, 16, 24), A.mult)
-        tt(S("vd"), V0n, S("DUMP"), A.subtract)
-        tt(S("t2b"), S("vd"), S("has"), A.mult)
-        dedupe("b", S("t2b"), "OB")
-        tt(v("TM", 0, m8), v("T1", 0, m8), v("pD", 0, m8), A.add)
+        tt(S("tk"), S("rc"), S("n2"), A.is_gt)
+        tt(nn, S("rc"), S("n2"), A.max)
+        tt(S("dvt"), S("dv"), S("tk"), A.mult)
+        tt(S("has"), nn, v(LM, 16, 24), A.min)
+        tt(V0n, V0, S("dvt"), A.add)
+        tt(S("t2b"), V0n, S("has"), A.mult)
+        dedupe(S("t2b"))
+        for b in range(8):
+            act(v("T1", b, m8, 8), v("RQ", b, m8, 8), AF.Copy, scale=S("zl", b))
         for b in range(8):
             ts(v("pK", b, m8, 8), v(LW, b, m8, 8), S("tk", b), A.mult)
+        tt(v("TM", 0, m8), v("T1", 0, m8), v("pD", 0, m8), A.add)
         tt(v("TM", 0, m8), v("TM", 0, m8), v("pK", 0, m8), A.add)
         ts(v("pA", 0, m8), v("TM", 0, m8), 0.0, A.is_equal)
         tt(v("pB", 0, m8), v("WA", 0, m8), v("pA", 0, m8), A.mult)
         tt(v(Wn, 0, m8), v("TM", 0, m8), v("pB", 0, m8), A.add)
-        dedupe1()
+        for b in range(8):
+            far(b)
+        for b in range(4, 8):
+            hit(b)
+        for b in range(8):
+            act(v("RX", b, m8, 8), v("E", b, m8, 8), AF.Identity, bias=S("k", b))
         for b in range(8):
             act(v("pJ", b, m8, 8), v("pS", b, m8, 8), AF.Copy, scale=S("tk", b))
         dedupe2(S("t2b"), "OB")
         tt(v("BS"), ind(xwin, v("OB")), v(LY, 0, 128), A.add)
+        tt(v(Rn, 0, m8), v("RX", 0, m8), v("pJ", 0, m8), A.add)
+        if t < ST - 1:
+            masks(t + 1)
+        else:
+            mm(v("pA", 0, 280), v("ID"), v(Rn, 8, 288), True, False)
+            mm(v("pA", 0, 280), v("IDN"), v(Rn, 0, 280), False, True)
+            mm(v("pY", 0, 288), v("ID"), v("PP"), True, False)
+            mm(v("pY", 0, 288), v("IDN"), v(Rn), False, True)
+            act(S("n5"), nn, AF.Copy, bias=-0.5)
+            for b in range(8):
+                act(v("SP", b, 288, 8), v(Rn, b, 288, 8), AF.Sign, bias=S("n5", b), scale=-1.0)
+            act(v("pB", 0, 288), v("SP"), AF.Relu)
+            act(v("T1", 0, 280), v("pA", 0, 280), AF.Sign)
         ts(v("BO"), v("BS"), 0.5, A.mult, -0.25, A.add)
         tc(ind(xwin, v("OB")), v("BO"))
         if t < ST - 1:
             lists(t + 1)
-        tt(v(Rn, 0, m8), v("RX", 0, m8), v("pJ", 0, m8), A.add)
 
     lists(0)
+    tc(S("n0"), v("NR"))
     for t in range(ST):
         step(t)
 
     so = [dma("s", T.yx[:, 0:2048], ap(v("X", 0, 2048)), [], [v("X", 0, 2048)]),
           dma("a", T.yx[:, 2048:4096], ap(v("X", 2048, 4096)), [], [v("X", 2048, 4096)]),
           dma("s", T.yn[:], ap(S("n4")), [], [S("n4")])]
-    n = S("n4")
     ms(v("T1", 280, 288), 1.0)
-    tt(v("T1", 0, 280), v("R4", 0, 280), v("R4", 8, 288), A.not_equal)
-    for b in range(8):
-        ts(v("pA", b, 288, 8), v("R4", b, 288, 8), S("n4", b), A.is_lt)
-    tt(v("E"), v("T1"), v("pA", 0, 288), A.mult)
     ts(v("U"), v("W4"), float(BIG), A.add)
+    tt(v("E"), v("T1"), v("pB", 0, 288), A.mult)
+    tt(v("DLT"), v("E"), v("pY", 0, 288), A.mult)
     tt(v("U"), v("U"), v("E"), A.mult)
-    tt(v("CV"), v("PP"), v("R4"), A.subtract)
-    tt(v("DLT"), v("CV"), v("E"), A.mult)
     for i in range(6):
         lo = 8 << i
         w = 288 - lo
         ts(v("BIT", lo, 288), v("DLT", lo, 288), i, A.arith_shift_right, 1, A.bitwise_and)
         tc(v("pA", lo, 288), v("BIT", lo, 288))
         tt(v("pB", lo, 288), v("U", lo, 288), v("pA", lo, 288), A.mult)
-        tt(v("pK", lo, 288), v("DLT", lo, 288), v("pA", lo, 288), A.mult)
+        if i < 5:
+            tt(v("pK", lo, 288), v("DLT", lo, 288), v("pA", lo, 288), A.mult)
         tt(v("U", lo, 288), v("U", lo, 288), v("pB", lo, 288), A.subtract)
-        tt(v("DLT", lo, 288), v("DLT", lo, 288), v("pK", lo, 288), A.subtract)
+        if i < 5:
+            tt(v("DLT", lo, 288), v("DLT", lo, 288), v("pK", lo, 288), A.subtract)
         tt(v("U", 0, w), v("U", 0, w), v("pB", lo, 288), A.add)
-        tt(v("DLT", 0, w), v("DLT", 0, w), v("pK", lo, 288), A.add)
-    tc(v("RT"), v("U", 0, 256))
+        if i < 5:
+            tt(v("DLT", 0, w), v("DLT", 0, w), v("pK", lo, 288), A.add)
     tc(v("RU", 0, 128), v("U", 128, 256))
     tc(v("RU", 128, 256), v("U", 0, 128))
-    turn(None, v("OI", 0, 256, 2), v("OI", 1, 256, 2))
+    turn("U", v("OI", 0, 256, 2), v("OI", 1, 256, 2))
     ts(v("VI", 0, 256), v("OI"), 12, A.arith_shift_right)
     tc(v("OV"), v("VI", 0, 256))
     so.append(dma("s", T.yv[:], ap(v("OV")), [], [v("OV")]))

@@ -8,6 +8,10 @@ N = 6
 ST = 4
 BIG = 16777216
 NX = 4224
+NV = 5
+SLACK = 0.03
+HA = 21
+GCS = (8, 17, 26)
 
 SCRATCH = {}
 
@@ -20,8 +24,8 @@ def _add(where, dtype, names, cols, rows=128):
 _add("sbuf", "bfloat16", "X", NX)
 _add("sbuf", "bfloat16", "XV H D AB", 4480)
 _add("sbuf", "int32", "W0 W1 W2 W3 W4 LW0 LW1 LW2 LW3 VI CI DLT BIT", 288)
-_add("sbuf", "bfloat16", "R0 R1 R2 R3 R4 QT ZERO ONES INV MK PP", 288)
-_add("sbuf", "float32", "POS Z Z0 DW RQ LX OA SP GG PZ WA RA A2 E T1 TM RX U", 288)
+_add("sbuf", "bfloat16", "R0 R1 R2 R3 R4 QT ZERO ONES INV MK PP XB A1 A2 RX TDR", 288)
+_add("sbuf", "float32", "POS Z Z0 RQ LX OA SP GG PZ WA E T1 TM U", 288)
 _add("sbuf", "uint16", "VL CL", 288)
 _add("sbuf", "uint16", "JL OL OB", 8)
 _add("sbuf", "bfloat16", "YR0 YR1 YR2 YR3 LY0 LY1 LY2 LY3", 416)
@@ -85,7 +89,86 @@ def rank_program(g, core, T, topo):
     def covers(x, y):
         return x[3] == 1 and x[1] <= y[1] and x[2] >= y[2] and x[4] <= y[4] and x[5] >= y[5]
 
-    def emit(eng, call, writes, reads, tok=None, inc=1, note=True):
+    ops, dacc, phase = [], {n: [] for n in SCRATCH}, {n: [] for n in SCRATCH}
+    LAT = 0.06
+
+    def emit(eng, call, writes, reads, tok=None, inc=1, note=True, cost=0.1, tail=0.0):
+        ws = [w[1] if w[0] == "ind" else w for w in writes]
+        rs = [w[2] for w in writes if w[0] == "ind"]
+        for w in reads:
+            if w[0] == "ind":
+                rs.append(w[1]); rs.append(w[2])
+            elif isinstance(w, tuple):
+                rs.append(w)
+        me, deps = len(ops), {}
+        for lst, wr in ((rs, False), (ws, True)):
+            for w in lst:
+                psum = w[0][0] == "p"
+                for (i, w2, wr2) in dacc[w[0]]:
+                    e2 = ops[i][0]
+                    if (wr or wr2) and (meets(w, w2) or (psum and eng == "t" and e2 == "t")):
+                        deps[i] = max(deps.get(i, 0.0), 0.0 if psum and e2 == eng == "t" else LAT)
+                if psum:
+                    ph = phase[w[0]]
+                    if ph and ph[-1][0] == eng:
+                        prev = ph[-2][1] if len(ph) > 1 else []
+                        ph[-1][1].append(me)
+                    else:
+                        prev = ph[-1][1] if ph else []
+                        ph.append([eng, [me]])
+                    for i in prev:
+                        deps[i] = LAT
+        deps.pop(me, None)
+        for w in rs:
+            dacc[w[0]].append((me, w, False))
+        for w in ws:
+            dacc[w[0]] = [x for x in dacc[w[0]] if not covers(w, x[1])] + [(me, w, True)]
+        ops.append((eng, call, writes, reads, tok, inc, note, cost, tail, deps))
+
+    def flush():
+        n = len(ops)
+        succ = [[] for _ in range(n)]
+        for i, o in enumerate(ops):
+            for d in o[9]:
+                succ[d].append((i, o[9][d]))
+        pri = [0.0] * n
+        for i in range(n - 1, -1, -1):
+            o = ops[i]
+            pri[i] = o[7] + max([o[8] + l + pri[s] for s, l in succ[i]] + [0.0])
+        left = [len(o[9]) for o in ops]
+        ready = {e: [] for e in list(Q) + ["x"]}
+        avail = [0.0] * n
+        for i in range(n):
+            if not left[i]:
+                ready[ops[i][0]].append(i)
+        free = {e: 0.0 for e in ready}
+        order, done = [], 0
+        while done < n:
+            best = None
+            for e in ready:
+                if ready[e]:
+                    t0 = max(free[e], min(avail[i] for i in ready[e]))
+                    if best is None or t0 < best[0]:
+                        best = (t0, e)
+            t0, e = best
+            i = max((i for i in ready[e] if avail[i] <= t0 + SLACK), key=lambda i: (pri[i], -i))
+            ready[e].remove(i)
+            st = max(t0, avail[i])
+            fin = st + ops[i][7]
+            if e != "x":
+                free[e] = fin
+            order.append((st, i))
+            done += 1
+            for s, l in succ[i]:
+                avail[s] = max(avail[s], fin + ops[i][8] + l)
+                left[s] -= 1
+                if not left[s]:
+                    ready[ops[s][0]].append(s)
+        for st, i in order:
+            if ops[i][0] != "x":
+                issue(*ops[i][:7])
+
+    def issue(eng, call, writes, reads, tok=None, inc=1, note=True):
         ws, rs = [], []
         for w in writes:
             if w[0] == "ind":
@@ -107,7 +190,7 @@ def rank_program(g, core, T, topo):
                     if psum and not same:
                         hit = True
                     elif same:
-                        hit = wr2 and not wr and meets(w, w2)
+                        hit = (wr or wr2) and meets(w, w2) and not (psum and eng == "t")
                     else:
                         hit = (wr or wr2) and meets(w, w2)
                     if hit and clk[eng].get(tk[0], 0) < tk[1] and need.get(tk[0], (0,))[0] < tk[1]:
@@ -148,48 +231,70 @@ def rank_program(g, core, T, topo):
     def sc(x):
         return ap(x) if isinstance(x, tuple) else x
 
+    def width(w):
+        if w[0] == "ind":
+            return 16 * (w[2][2] - w[2][1])
+        return (w[2] - w[1] + w[3] - 1) // w[3]
+
+    def us(o, ins, rate, fix=0.0, gather=1.56):
+        if o[0] == "ind":
+            return 0.05 + 3.5 * width(o) * 0.00083
+        if any(x[0] == "ind" for x in ins):
+            return 0.05 + gather * width(o) * 0.00083
+        return max(64, max(width(x) for x in ins) * rate) * 0.00083 + fix
+
+    def small(*vs):
+        return 0.5 if all(x[0] != "ind" and x[0][0] != "p" and SCRATCH[x[0]][2] in ("bfloat16", "uint16") for x in vs) else 1
+
     def tc(o, i):
-        emit("v", lambda: g.vector.tensor_copy(ap(o), ap(i)), [o], [i])
+        emit("v", lambda: g.vector.tensor_copy(ap(o), ap(i)), [o], [i], cost=us(o, [i], small(o, i)))
 
     def tt(o, x, y, op):
-        emit("v", lambda: g.vector.tensor_tensor(ap(o), ap(x), ap(y), op), [o], [x, y])
+        emit("v", lambda: g.vector.tensor_tensor(ap(o), ap(x), ap(y), op), [o], [x, y],
+             cost=us(o, [x, y], 1 if "p" in (x[0][0], y[0][0]) else 2))
 
     def ts(o, x, s1, op0, s2=None, op1=None):
         r = [x] + [s for s in (s1, s2) if isinstance(s, tuple)]
+        c = us(o, [x], small(o, x))
         if op1 is None:
-            emit("v", lambda: g.vector.tensor_scalar(ap(o), ap(x), sc(s1), None, op0), [o], r)
+            emit("v", lambda: g.vector.tensor_scalar(ap(o), ap(x), sc(s1), None, op0), [o], r, cost=c)
         else:
-            emit("v", lambda: g.vector.tensor_scalar(ap(o), ap(x), sc(s1), sc(s2), op0, op1), [o], r)
+            emit("v", lambda: g.vector.tensor_scalar(ap(o), ap(x), sc(s1), sc(s2), op0, op1), [o], r, cost=c)
 
     def tr(o, x, op, ab=False):
-        emit("v", lambda: g.vector.tensor_reduce(ap(o), ap(x), AxisListType.X, op, apply_absolute_value=ab), [o], [x])
+        emit("v", lambda: g.vector.tensor_reduce(ap(o), ap(x), AxisListType.X, op, apply_absolute_value=ab), [o], [x],
+             cost=us(o, [x], 1))
 
     def ms(o, c):
-        emit("v", lambda: g.vector.memset(ap(o), c), [o], [])
+        emit("v", lambda: g.vector.memset(ap(o), c), [o], [], cost=us(o, [o], 1))
 
     def tp(o, x):
-        emit("v", lambda: g.vector.transpose(ap(o), ap(x)), [o], [x])
+        emit("v", lambda: g.vector.transpose(ap(o), ap(x)), [o], [x], cost=us(o, [x], 1))
 
     def act(o, x, f, bias=None, scale=1.0):
         r = [x] + [s for s in (bias, scale) if isinstance(s, tuple)]
+        c = us(o, [x], 1)
         if bias is None:
-            emit("a", lambda: g.scalar.activation(ap(o), ap(x), f, scale=sc(scale)), [o], r)
+            emit("a", lambda: g.scalar.activation(ap(o), ap(x), f, scale=sc(scale)), [o], r, cost=c)
         else:
-            emit("a", lambda: g.scalar.activation(ap(o), ap(x), f, bias=sc(bias), scale=sc(scale)), [o], r)
+            emit("a", lambda: g.scalar.activation(ap(o), ap(x), f, bias=sc(bias), scale=sc(scale)), [o], r, cost=c)
 
     def mm(o, l, r, start, stop):
-        emit("t", lambda: g.tensor.matmul(ap(o), ap(l), ap(r), start, stop), [o], [l, r])
+        c = max(64, width(r)) * 0.00083 * (4 if SCRATCH[r[0]][2] == "float32" else 1)
+        emit("t", lambda: g.tensor.matmul(ap(o), ap(l), ap(r), start, stop), [o], [l, r], cost=c)
 
     def iota(o, pat, base, cm):
+        c = 0.13 + 2 * width(o) * 0.00083
         if SCRATCH[o[0]][2] == "int32":
-            emit("p", lambda: g.iota(ap(o), pat, base, cm), [o], [])
+            emit("p", lambda: g.iota(ap(o), pat, base, cm), [o], [], cost=c)
         else:
-            emit("p", lambda: g.iota(ap(o), pat, base, cm, allow_small_or_imprecise_dtypes=True), [o], [])
+            emit("p", lambda: g.iota(ap(o), pat, base, cm, allow_small_or_imprecise_dtypes=True), [o], [], cost=c)
 
     def dma(eng, out, in_, writes, reads):
         s = "d%d" % nd[0]
         nd[0] += 1
-        emit(eng, lambda: Q[eng].dma_start(out, in_), writes, reads, tok=(s, 16), inc=16)
+        emit(eng, lambda: Q[eng].dma_start(out, in_), writes, reads, tok=(s, 16), inc=16,
+             tail=2.0 + sum(width(w) for w in writes) * 128 * 2 / 200e3)
         return s
 
     scol = {}
@@ -211,7 +316,9 @@ def rank_program(g, core, T, topo):
         rid, pid, _e = topo.addr(to)
         m = topo.mask(core, to)
         o, i = v(dst, 0, width), v(src, 0, width)
-        emit("p", lambda: g.remote_dma(ap(o), ap(i), T.sem[sem], T.sem.ls, pid, rid, m), [], [i], note=False)
+        emit("p", lambda: g.remote_dma(ap(o), ap(i), T.sem[sem], T.sem.ls, pid, rid, m), [], [i], note=False, cost=0.6)
+        ops.append(("x", None, [], [], None, 0, False, 0.0, 0.0, {len(ops) - 1: 3.0}))
+        dacc[dst].append((len(ops) - 1, v(dst, 0, width), True))
         cnt["ls"] += len(topo.engines(core, to))
 
     dma("s", ap(v("VR")), T.vl[:], [v("VR")], [])
@@ -259,6 +366,7 @@ def rank_program(g, core, T, topo):
             ms(v("R%d" % t, 256 + 8 * t, 264 + 8 * t), 64.0)
     ms(v("X", 4096, NX), 0.0)
     ms(v("ZERO"), 0.0)
+    ms(v("XB", 0, 8), 0.0)
     ms(v("ONES"), 1.0)
 
     def turn(raw, w0, w1):
@@ -319,12 +427,12 @@ def rank_program(g, core, T, topo):
 
     def masks(t):
         R, G8 = "R%d" % t, (30 + t) * 8
-        mm(v("pA", 0, G8), v("ID"), v(R, 8, G8 + 8), True, False)
-        mm(v("pA", 0, G8), v("IDN"), v(R, 0, G8), False, True)
+        mm(v("pI", 0, G8), v("ID"), v(R, 8, G8 + 8), True, False)
+        mm(v("pI", 0, G8), v("IDN"), v(R, 0, G8), False, True)
         act(S("b25"), S("n%d" % t), AF.Copy, bias=2.5, scale=-1.0)
         for b in range(8):
             act(v("INV", b, G8, 8), v(R, b, G8, 8), AF.Sign, bias=S("b25", b))
-        act(v("MK", 0, G8), v("pA", 0, G8), AF.Relu, bias=1.0, scale=-1.0)
+        act(v("MK", 0, G8), v("pI", 0, G8), AF.Relu, bias=1.0, scale=-1.0)
 
     def dedupe(t2):
         mm(v("pI", 0, 128), v("BLK"), v("EXC"), True, False)
@@ -340,14 +448,14 @@ def rank_program(g, core, T, topo):
     def hit(b):
         x, o = v("AA", b * 128, b * 128 + 128), v("AB", b * 128, b * 128 + 128)
         emit("a", lambda: g.scalar.activation(ap(o), ap(x), AF.Relu, bias=ap(S("HI", b)), scale=-1.0, accum_out=ap(S("hit", b))),
-             [o, S("hit", b)], [x, S("HI", b)])
+             [o, S("hit", b)], [x, S("HI", b)], cost=0.126)
 
     def half(nm, k):
         c = S(nm)[1]
-        return v("SM", c + 4 * k, c + 4 * k + 4)
+        return v("SM", c + NV * k, c + (8 if k else NV))
 
     def dedupe2(t2, off):
-        for b in range(4):
+        for b in range(NV):
             tr(S("mn", b), v("AA", b * 128, b * 128 + 128), A.min)
         tt(half("nd", 0), half("mn", 0), half("THR", 0), A.is_gt)
         ts(half("nd", 1), half("hit", 1), 0.0, A.is_equal)
@@ -370,8 +478,9 @@ def rank_program(g, core, T, topo):
         for buf, sem, wd in ((LW, "aw", m8), (LY, "ay", 128 + m8), (LM, "am", 24)):
             record((sem + str(t), ne), [v(buf, 0, wd)], [], {})
 
-        gc = [(0, 8), (8, 17), (17, 26), (26, G)]
-        vc = [(0, 9), (9, 18), (18, 27), (27, P)]
+        c1, c2, c3 = GCS
+        gc = [(0, c1), (c1, c2), (c2, c3), (c3, G)]
+        vc = [(0, c1 + 1), (c1 + 1, c2 + 1), (c2 + 1, c3 + 1), (c3 + 1, P)]
 
         def gv(c):
             r0, r1 = vc[c]
@@ -386,10 +495,15 @@ def rank_program(g, core, T, topo):
 
         def idp(c):
             for k, (r0, r1) in enumerate(hs(c)):
-                mm(v(hb[k], 0, (r1 - r0) * 128), v("ID"), v("XV", r0 * 128, r1 * 128), True, True)
+                mm(v(hb[k], 0, (r1 - r0) * 128), v("ID"), v("XV", r0 * 128, r1 * 128), True, r0 < HA)
+                if r0 >= HA:
+                    mm(v(hb[k], 0, (r1 - r0) * 128), v("ID"), v("XV", r0 * 128 + 128, r1 * 128 + 128), False, True)
 
         def hh(c):
             for k, (r0, r1) in enumerate(hs(c)):
+                if r0 >= HA:
+                    act(v("H", r0 * 128, r1 * 128), v(hb[k], 0, (r1 - r0) * 128), AF.Copy)
+                    continue
                 tt(v("H", r0 * 128, r1 * 128), v("XV", r0 * 128 + 128, r1 * 128 + 128), v(hb[k], 0, (r1 - r0) * 128), A.add)
 
         def dd(c):
@@ -422,28 +536,28 @@ def rank_program(g, core, T, topo):
         hh(0)
         dd(0)
         idp(1)
-        sums("pD", "WBM", "XV", 0, 9, False)
+        sums("pD", "WBM", "XV", 0, c1 + 1, False)
         hh(1)
         idp(2)
-        sums("pD", "WBM", "XV", 9, 18, False)
+        sums("pD", "WBM", "XV", c1 + 1, c2 + 1, False)
         aba(0)
-        sums("pK", "WBK", "AB", 0, 8, False)
+        sums("pK", "WBK", "AB", 0, c1, False)
         gv(3)
         dd(1)
         hh(2)
         idp(3)
-        sums("pD", "WBM", "XV", 18, 27, False)
+        sums("pD", "WBM", "XV", c2 + 1, c3 + 1, False)
         aba(1)
-        sums("pK", "WBK", "AB", 8, 17, False)
+        sums("pK", "WBK", "AB", c1, c2, False)
         dd(2)
         hh(3)
         aba(2)
-        sums("pK", "WBK", "AB", 17, 26, False)
+        sums("pK", "WBK", "AB", c2, c3, False)
         dd(3)
         aba(3)
         sums("pK", "WBK", "AB", gc[3][0], G, True)
-        sums("pD", "WBM", "XV", 27, P, False)
-        tt(v("DW", 8, m8), v(W, 0, n8), v(W, 8, m8), A.subtract)
+        sums("pD", "WBM", "XV", c3 + 1, P, False)
+        tt(v("pJ", 8, m8), v(W, 0, n8), v(W, 8, m8), A.subtract)
         if t:
             cj = v("SI", 236, 237)
             tc(cj, v("pS", 400, 401))
@@ -455,8 +569,7 @@ def rank_program(g, core, T, topo):
             scalar_constants()
 
         for b in range(8):
-            tr(S("mx", b), v("pK", b, G8, 8), A.max)
-        tc(J("mx"), S("mx"))
+            tr(v("SI", J("mx")[1] + b, J("mx")[1] + b + 1), v("pK", b, G8, 8), A.max)
         ts(J("q"), J("mx"), 8064, A.bitwise_and)
         tt(S("jk"), S("BA"), J("q"), A.subtract)
         tc(v("JL"), S("jk"))
@@ -468,11 +581,11 @@ def rank_program(g, core, T, topo):
             ts(v("pY", k * 128, k * 128 + 128), Y, 0.5, A.mult)
         ts(J("k"), J("mx"), 127, A.bitwise_and)
         tc(S("k"), J("k"))
+        ts(S("bO"), J("mx"), -1.0 / 128, A.mult, 0.5, A.add)
         act(S("nk"), S("k"), AF.Copy, bias=-1.0, scale=-1.0)
         act(S("k15"), S("k"), AF.Copy, bias=1.5)
         act(S("kn"), S("k"), AF.Copy, scale=-1.0)
         act(v(M, 16, 24), S("L"), AF.Copy)
-        act(S("bO"), S("mx"), AF.Copy, bias=0.5, scale=-1.0 / 128)
         act(S("jb"), S("jk"), AF.Copy, bias=-0.5, scale=-1.0)
         act(S("jb1"), S("jk"), AF.Copy, bias=-128.0, scale=-1.0)
         for b in range(8):
@@ -513,8 +626,7 @@ def rank_program(g, core, T, topo):
         tt(S("nk1"), n, S("nk"), A.add)
         tt(v("PZ", 0, G8), v("pB", 0, G8), v("Z", 0, G8), A.mult)
         for b in range(8):
-            tr(S("z", b), v("PZ", b, G8, 8), A.min)
-        tc(J("z"), S("z"))
+            tr(v("SI", J("z")[1] + b, J("z")[1] + b + 1), v("PZ", b, G8, 8), A.min)
         ts(J("vk"), J("z"), 12, A.arith_shift_right, 4095, A.bitwise_and)
         ts(J("vk1"), J("z"), 4095, A.bitwise_and)
         tt(v(M, 8, 16), J("vk1"), S("DUMP"), A.subtract)
@@ -523,9 +635,8 @@ def rank_program(g, core, T, topo):
         for b in range(8):
             tr(S("vm", b), v("PZ", b, n8, 8), A.max)
         ts(S("cl"), S("vm"), 0.0, A.is_gt)
-        ts(S("vp"), S("vm"), 0.0, A.max)
         tt(S("sz0"), S("cl"), S("nk1"), A.mult)
-        tt(v(M, 0, 8), S("sz0"), S("vp"), A.subtract)
+        tt(v(M, 0, 8), S("sz0"), S("vm"), A.subtract)
         sz = v(M, 0, 8)
         send(M, LM, 24, "am%d" % t, to)
         tt(S("gr"), S("L"), S("cl"), A.subtract)
@@ -547,29 +658,30 @@ def rank_program(g, core, T, topo):
         tt(S("wn"), S("wn1"), S("gr"), A.mult)
         for b in range(8):
             act(v("pD", b, m8, 8), v("OA", b, m8, 8), AF.Copy, scale=S("wn", b))
-        tt(v("pA", 8, m8), v("GG", 8, m8), v("pY", 8, m8), A.mult)
-        tt(v("pB", 8, m8), v("GG", 8, m8), v("DW", 8, m8), A.mult)
-        tt(v("RA", 8, m8), v(R, 8, m8), v("pA", 8, m8), A.add)
+        tt(v("XB", 8, m8), v("GG", 8, m8), v("pY", 8, m8), A.mult)
+        mm(v("pA", 0, m8), v("ID"), v(R, 0, m8), True, False)
+        mm(v("pA", 0, m8), v("ID"), v("XB", 0, m8), False, True)
+        tt(v("pB", 8, m8), v("GG", 8, m8), v("pJ", 8, m8), A.mult)
         tt(v("WA", 8, m8), v(W, 8, m8), v("pB", 8, m8), A.add)
-        tc(v("RA", 0, 8), v(R, 0, 8))
         tc(v("WA", 0, 8), v(W, 0, 8))
         tt(S("kns"), S("kn"), sz, A.subtract)
-        tt(S("zl"), S("z"), S("L"), A.mult)
+        tt(S("zl"), J("z"), S("L"), A.mult)
         act(v("YX", 0, 8), S("cl"), AF.Copy)
         act(S("rest"), S("L"), AF.Copy, bias=1.0, scale=-1.0)
         for b in range(8):
             far(b)
-        for b in range(4, 8):
+        for b in range(NV, 8):
             hit(b)
         for b in range(8):
-            act(v("pA", b, m8, 8), v("RA", b, m8, 8), AF.Relu, bias=S("kns", b))
+            act(v("A1", b, m8, 8), v("pA", b, m8, 8), AF.Relu, bias=S("kns", b))
         tt(S("ng"), n, S("gr"), A.add)
         ts(S("ng"), S("ng"), 32.0, A.min)
         tt(S("n2"), S("ng"), sz, A.subtract)
         dedupe2(S("t2g"), "OL")
         tc(ind(xwin, v("OL")), Y)
-        tt(v("E", 0, m8), v("pA", 0, m8), v("A2", 0, m8), A.subtract)
-        act(v("RQ", 0, m8), v("E", 0, m8), AF.Abs)
+        mm(v("pA", 0, m8), v("ID"), v("A1", 0, m8), True, False)
+        mm(v("pA", 0, m8), v("IDN"), v("A2", 0, m8), False, True)
+        act(v("RQ", 0, m8), v("pA", 0, m8), AF.Abs)
         act(v("RQ", 0, m8), v("RQ", 0, m8), AF.Relu, bias=1.0, scale=-1.0)
         mm(v("pS", 0, m8), v("ID"), v(LY, 128, 128 + m8), True, False)
         mm(v("pS", 0, m8), v("IDN"), v(R, 0, m8), False, True)
@@ -589,23 +701,25 @@ def rank_program(g, core, T, topo):
         for b in range(8):
             act(v("T1", b, m8, 8), v("RQ", b, m8, 8), AF.Copy, scale=S("zl", b))
         for b in range(8):
+            act(v("RX", b, m8, 8), v("pA", b, m8, 8), AF.Identity, bias=S("k", b))
+        for b in range(8):
             ts(v("pK", b, m8, 8), v(LW, b, m8, 8), S("tk", b), A.mult)
         tt(v("TM", 0, m8), v("T1", 0, m8), v("pD", 0, m8), A.add)
         tt(v("TM", 0, m8), v("TM", 0, m8), v("pK", 0, m8), A.add)
-        ts(v("pA", 0, m8), v("TM", 0, m8), 0.0, A.is_equal)
-        tt(v("pB", 0, m8), v("WA", 0, m8), v("pA", 0, m8), A.mult)
+        ts(v("pY", 0, m8), v("TM", 0, m8), 0.0, A.is_equal)
+        tt(v("pB", 0, m8), v("WA", 0, m8), v("pY", 0, m8), A.mult)
         tt(v(Wn, 0, m8), v("TM", 0, m8), v("pB", 0, m8), A.add)
         for b in range(8):
             far(b)
-        for b in range(4, 8):
+        for b in range(NV, 8):
             hit(b)
         for b in range(8):
-            act(v("RX", b, m8, 8), v("E", b, m8, 8), AF.Identity, bias=S("k", b))
-        for b in range(8):
-            act(v("pJ", b, m8, 8), v("pS", b, m8, 8), AF.Copy, scale=S("tk", b))
+            act(v("TDR", b, m8, 8), v("pS", b, m8, 8), AF.Copy, scale=S("tk", b))
+        mm(v("pJ", 0, m8), v("ID"), v("RX", 0, m8), True, False)
+        mm(v("pJ", 0, m8), v("ID"), v("TDR", 0, m8), False, True)
+        act(v(Rn, 0, m8), v("pJ", 0, m8), AF.Copy)
         dedupe2(S("t2b"), "OB")
         tt(v("BS"), ind(xwin, v("OB")), v(LY, 0, 128), A.add)
-        tt(v(Rn, 0, m8), v("RX", 0, m8), v("pJ", 0, m8), A.add)
         if t < ST - 1:
             masks(t + 1)
         else:
@@ -659,6 +773,7 @@ def rank_program(g, core, T, topo):
     ts(v("CI", 0, 256), v("OI"), 4095, A.bitwise_and)
     tc(v("OC"), v("CI", 0, 256))
     so.append(dma("a", T.yc[:], ap(v("OC")), [], [v("OC")]))
+    flush()
     for s in so:
         g.sync.wait_ge(T.sem[s], 16)
     for s in ("qv", "qa", "qt", "qp"):

import numpy as np
import comms_topo
from concourse.mybir import dt, AluOpType, AxisListType, ActivationFunctionType

A = AluOpType
AF = ActivationFunctionType
N = 6
ST = 4
BIG = 16777216
NX = 4224
NV = 5
SLACK = 0.03
HA = 21
GCS = (8, 17, 26)

SCRATCH = {}


def _add(where, dtype, names, cols, rows=128):
    for nm in names.split():
        SCRATCH[nm] = (where, [rows, cols], dtype)


_add("sbuf", "bfloat16", "X", NX)
_add("sbuf", "bfloat16", "XV H D AB", 4480)
_add("sbuf", "int32", "W0 W1 W2 W3 W4 LW0 LW1 LW2 LW3 VI CI DLT BIT", 288)
_add("sbuf", "bfloat16", "R0 R1 R2 R3 R4 QT ZERO ONES INV MK PP XB A1 A2 RX TDR", 288)
_add("sbuf", "float32", "POS Z Z0 RQ LX OA SP GG PZ WA E T1 TM U", 288)
_add("sbuf", "uint16", "VL CL", 288)
_add("sbuf", "uint16", "JL OL OB", 8)
_add("sbuf", "bfloat16", "YR0 YR1 YR2 YR3 LY0 LY1 LY2 LY3", 416)
_add("sbuf", "float32", "M0 M1 M2 M3 LM0 LM1 LM2 LM3", 24)
_add("sbuf", "float32", "SM", 720)
_add("sbuf", "int32", "SI", 240)
_add("sbuf", "float32", "ROWI", 143)
_add("sbuf", "bfloat16", "WB1 WBK WB4 WBM WBW", 143)
_add("sbuf", "bfloat16", "ID IDM IDH IDN DK TK BI YX", 128)
_add("sbuf", "float32", "BLK GB EX EXC", 128)
_add("sbuf", "int32", "CIO BO", 128)
_add("sbuf", "float32", "BS", 128)
_add("sbuf", "float32", "DG", 16)
_add("sbuf", "float32", "AA", 1024)
_add("sbuf", "int32", "VR CR", 256)
_add("sbuf", "float32", "RT RU TA TB TC TE OUT", 256)
_add("sbuf", "float32", "OV OC", 256)
_add("sbuf", "int32", "OI", 256)
_add("sbuf", "int32", "NR", 8)
_add("sbuf", "int32", "THR8", 1, 8)
_add("sbuf", "int32", "WT", 1)
_add("psum", "float32", "pA pB pK pD pY pS pI pJ", 512)

SEMAPHORES = ["qv", "qa", "qt", "qp", "ls"] + ["d%d" % i for i in range(12)] + [
    m + str(t) for m in ("aw", "ay", "am") for t in range(ST)]


def rank_program(g, core, T, topo):
    rank = T.rank_of(core)
    if rank is None:
        return
    Q = {"v": g.vector, "a": g.scalar, "t": g.tensor, "p": g, "s": g.sync}
    SEM = {"v": "qv", "a": "qa", "t": "qt", "p": "qp", "s": None}
    cnt = {"qv": 0, "qa": 0, "qt": 0, "qp": 0, "ls": 0}
    clk = {e: {} for e in Q}
    acc = {n: [] for n in SCRATCH}
    nd = [0]

    def v(name, lo=0, hi=None, step=1, p0=0, p1=None):
        sh = SCRATCH[name][1]
        return (name, lo, sh[1] if hi is None else hi, step, p0, sh[0] if p1 is None else p1)

    def ap(w):
        if w[0] == "ind":
            return ap(w[1]).indirect(ap(w[2]))
        n, lo, hi, st, p0, p1 = w
        if st == 1:
            return T[n][p0:p1, lo:hi]
        return T[n][p0:p1, lo:hi:st]

    def ind(win, off):
        return ("ind", win, off)

    def meets(x, y):
        if x[1] >= y[2] or y[1] >= x[2] or x[4] >= y[5] or y[4] >= x[5]:
            return False
        if x[3] == y[3] and x[3] > 1 and (x[1] - y[1]) % x[3]:
            return False
        return True

    def covers(x, y):
        return x[3] == 1 and x[1] <= y[1] and x[2] >= y[2] and x[4] <= y[4] and x[5] >= y[5]

    ops, dacc, phase = [], {n: [] for n in SCRATCH}, {n: [] for n in SCRATCH}
    LAT = 0.06

    def emit(eng, call, writes, reads, tok=None, inc=1, note=True, cost=0.1, tail=0.0):
        ws = [w[1] if w[0] == "ind" else w for w in writes]
        rs = [w[2] for w in writes if w[0] == "ind"]
        for w in reads:
            if w[0] == "ind":
                rs.append(w[1]); rs.append(w[2])
            elif isinstance(w, tuple):
                rs.append(w)
        me, deps = len(ops), {}
        for lst, wr in ((rs, False), (ws, True)):
            for w in lst:
                psum = w[0][0] == "p"
                for (i, w2, wr2) in dacc[w[0]]:
                    e2 = ops[i][0]
                    if (wr or wr2) and (meets(w, w2) or (psum and eng == "t" and e2 == "t")):
                        deps[i] = max(deps.get(i, 0.0), 0.0 if psum and e2 == eng == "t" else LAT)
                if psum:
                    ph = phase[w[0]]
                    if ph and ph[-1][0] == eng:
                        prev = ph[-2][1] if len(ph) > 1 else []
                        ph[-1][1].append(me)
                    else:
                        prev = ph[-1][1] if ph else []
                        ph.append([eng, [me]])
                    for i in prev:
                        deps[i] = LAT
        deps.pop(me, None)
        for w in rs:
            dacc[w[0]].append((me, w, False))
        for w in ws:
            dacc[w[0]] = [x for x in dacc[w[0]] if not covers(w, x[1])] + [(me, w, True)]
        ops.append((eng, call, writes, reads, tok, inc, note, cost, tail, deps))

    def flush():
        n = len(ops)
        succ = [[] for _ in range(n)]
        for i, o in enumerate(ops):
            for d in o[9]:
                succ[d].append((i, o[9][d]))
        pri = [0.0] * n
        for i in range(n - 1, -1, -1):
            o = ops[i]
            pri[i] = o[7] + max([o[8] + l + pri[s] for s, l in succ[i]] + [0.0])
        left = [len(o[9]) for o in ops]
        ready = {e: [] for e in list(Q) + ["x"]}
        avail = [0.0] * n
        for i in range(n):
            if not left[i]:
                ready[ops[i][0]].append(i)
        free = {e: 0.0 for e in ready}
        order, done = [], 0
        while done < n:
            best = None
            for e in ready:
                if ready[e]:
                    t0 = max(free[e], min(avail[i] for i in ready[e]))
                    if best is None or t0 < best[0]:
                        best = (t0, e)
            t0, e = best
            i = max((i for i in ready[e] if avail[i] <= t0 + SLACK), key=lambda i: (pri[i], -i))
            ready[e].remove(i)
            st = max(t0, avail[i])
            fin = st + ops[i][7]
            if e != "x":
                free[e] = fin
            order.append((st, i))
            done += 1
            for s, l in succ[i]:
                avail[s] = max(avail[s], fin + ops[i][8] + l)
                left[s] -= 1
                if not left[s]:
                    ready[ops[s][0]].append(s)
        for st, i in order:
            if ops[i][0] != "x":
                issue(*ops[i][:7])

    def issue(eng, call, writes, reads, tok=None, inc=1, note=True):
        ws, rs = [], []
        for w in writes:
            if w[0] == "ind":
                ws.append(w[1]); rs.append(w[2])
            else:
                ws.append(w)
        for w in reads:
            if w[0] == "ind":
                rs.append(w[1]); rs.append(w[2])
            elif isinstance(w, tuple):
                rs.append(w)
        mysem = tok[0] if tok else SEM[eng]
        need = {}
        for lst, wr in ((rs, False), (ws, True)):
            for w in lst:
                psum = w[0][0] == "p"
                for (tk, w2, wr2, ck2) in acc[w[0]]:
                    same = tk[0] == mysem
                    if psum and not same:
                        hit = True
                    elif same:
                        hit = (wr or wr2) and meets(w, w2) and not (psum and eng == "t")
                    else:
                        hit = (wr or wr2) and meets(w, w2)
                    if hit and clk[eng].get(tk[0], 0) < tk[1] and need.get(tk[0], (0,))[0] < tk[1]:
                        need[tk[0]] = (tk[1], ck2)
        ck = clk[eng]
        for s in list(need):
            val, c2 = need[s]
            if any(s2 != s and need[s2][1].get(s, 0) >= val for s2 in need):
                continue
            Q[eng].wait_ge(T.sem[s], val)
            for k2 in c2:
                ck[k2] = max(ck.get(k2, 0), c2[k2])
            ck[s] = max(ck.get(s, 0), val)
        ins = call()
        if not note:
            return None
        if tok is None:
            cnt[mysem] += 1
            tok = (mysem, cnt[mysem])
        ins.then_inc(T.sem[tok[0]], inc)
        snap = dict(ck)
        snap[tok[0]] = tok[1]
        record(tok, ws, rs, snap)
        return tok

    def record(tok, ws, rs, snap):
        for w in rs:
            old = acc[w[0]]
            if w[0][0] == "p":
                old = [x for x in old if x[0][0] == tok[0]]
            acc[w[0]] = [x for x in old if not (x[0][0] == tok[0] and not x[2] and covers(w, x[1]))] + [(tok, w, False, snap)]
        for w in ws:
            old = acc[w[0]]
            if w[0][0] == "p":
                old = [x for x in old if x[0][0] == tok[0]]
            acc[w[0]] = [x for x in old if not covers(w, x[1])] + [(tok, w, True, snap)]

    def sc(x):
        return ap(x) if isinstance(x, tuple) else x

    def width(w):
        if w[0] == "ind":
            return 16 * (w[2][2] - w[2][1])
        return (w[2] - w[1] + w[3] - 1) // w[3]

    def us(o, ins, rate, fix=0.0, gather=1.56):
        if o[0] == "ind":
            return 0.05 + 3.5 * width(o) * 0.00083
        if any(x[0] == "ind" for x in ins):
            return 0.05 + gather * width(o) * 0.00083
        return max(64, max(width(x) for x in ins) * rate) * 0.00083 + fix

    def small(*vs):
        return 0.5 if all(x[0] != "ind" and x[0][0] != "p" and SCRATCH[x[0]][2] in ("bfloat16", "uint16") for x in vs) else 1

    def tc(o, i):
        emit("v", lambda: g.vector.tensor_copy(ap(o), ap(i)), [o], [i], cost=us(o, [i], small(o, i)))

    def tt(o, x, y, op):
        emit("v", lambda: g.vector.tensor_tensor(ap(o), ap(x), ap(y), op), [o], [x, y],
             cost=us(o, [x, y], 1 if "p" in (x[0][0], y[0][0]) else 2))

    def ts(o, x, s1, op0, s2=None, op1=None):
        r = [x] + [s for s in (s1, s2) if isinstance(s, tuple)]
        c = us(o, [x], small(o, x))
        if op1 is None:
            emit("v", lambda: g.vector.tensor_scalar(ap(o), ap(x), sc(s1), None, op0), [o], r, cost=c)
        else:
            emit("v", lambda: g.vector.tensor_scalar(ap(o), ap(x), sc(s1), sc(s2), op0, op1), [o], r, cost=c)

    def tr(o, x, op, ab=False):
        emit("v", lambda: g.vector.tensor_reduce(ap(o), ap(x), AxisListType.X, op, apply_absolute_value=ab), [o], [x],
             cost=us(o, [x], 1))

    def ms(o, c):
        emit("v", lambda: g.vector.memset(ap(o), c), [o], [], cost=us(o, [o], 1))

    def tp(o, x):
        emit("v", lambda: g.vector.transpose(ap(o), ap(x)), [o], [x], cost=us(o, [x], 1))

    def act(o, x, f, bias=None, scale=1.0):
        r = [x] + [s for s in (bias, scale) if isinstance(s, tuple)]
        c = us(o, [x], 1)
        if bias is None:
            emit("a", lambda: g.scalar.activation(ap(o), ap(x), f, scale=sc(scale)), [o], r, cost=c)
        else:
            emit("a", lambda: g.scalar.activation(ap(o), ap(x), f, bias=sc(bias), scale=sc(scale)), [o], r, cost=c)

    def mm(o, l, r, start, stop):
        c = max(64, width(r)) * 0.00083 * (4 if SCRATCH[r[0]][2] == "float32" else 1)
        emit("t", lambda: g.tensor.matmul(ap(o), ap(l), ap(r), start, stop), [o], [l, r], cost=c)

    def iota(o, pat, base, cm):
        c = 0.13 + 2 * width(o) * 0.00083
        if SCRATCH[o[0]][2] == "int32":
            emit("p", lambda: g.iota(ap(o), pat, base, cm), [o], [], cost=c)
        else:
            emit("p", lambda: g.iota(ap(o), pat, base, cm, allow_small_or_imprecise_dtypes=True), [o], [], cost=c)

    def dma(eng, out, in_, writes, reads):
        s = "d%d" % nd[0]
        nd[0] += 1
        emit(eng, lambda: Q[eng].dma_start(out, in_), writes, reads, tok=(s, 16), inc=16,
             tail=2.0 + sum(width(w) for w in writes) * 128 * 2 / 200e3)
        return s

    scol = {}
    jcol = {}

    def S(nm, b=None):
        if nm not in scol:
            scol[nm] = 8 * len(scol)
        c = scol[nm]
        return v("SM", c, c + 8) if b is None else v("SM", c + b, c + b + 1)

    def J(nm):
        if nm not in jcol:
            jcol[nm] = 8 * len(jcol)
        c = jcol[nm]
        return v("SI", c, c + 8)

    def send(src, dst, width, sem, to):
        rid, pid, _e = topo.addr(to)
        m = topo.mask(core, to)
        o, i = v(dst, 0, width), v(src, 0, width)
        emit("p", lambda: g.remote_dma(ap(o), ap(i), T.sem[sem], T.sem.ls, pid, rid, m), [], [i], note=False, cost=0.6)
        ops.append(("x", None, [], [], None, 0, False, 0.0, 0.0, {len(ops) - 1: 3.0}))
        dacc[dst].append((len(ops) - 1, v(dst, 0, width), True))
        cnt["ls"] += len(topo.engines(core, to))

    dma("s", ap(v("VR")), T.vl[:], [v("VR")], [])
    dma("a", ap(v("CR")), T.cl[:], [v("CR")], [])
    dma("a", ap(v("X", 2048, 4096)), T.xc[:, 2048:4096], [v("X", 2048, 4096)], [])
    dma("s", ap(v("X", 0, 2048)), T.xc[:, 0:2048], [v("X", 0, 2048)], [])
    dma("s", ap(v("NR")), T.ln[:], [v("NR")], [])
    dma("a", ap(v("THR8")), T.th[:], [v("THR8")], [])
    dma("a", ap(v("WT")), T.wt[:], [v("WT")], [])

    pi = v("SI", 232, 233)
    pg = v("SI", 233, 234)
    pa = v("SI", 234, 235)
    pp = v("SI", 235, 236)
    iota(pi, [[1, 1]], 0, 1)
    iota(v("ROWI"), [[1, 143]], -15, 0)
    iota(v("CIO"), [[1, 128]], 0, 0)
    iota(S("BA"), [[16, 8]], 8064, 0)
    iota(S("B8"), [[1, 8]], 0, 0)
    iota(v("R0", 0, 256), [[1, 32], [0, 8]], 0, 0)
    iota(v("R0", 256, 288), [[0, 4], [0, 8]], 64, 0)
    iota(v("QT"), [[-128, 36], [0, 8]], 8064, 0)
    iota(v("POS"), [[128, 36], [16, 8]], 0, 0)
    iota(v("PP"), [[1, 36], [0, 8]], 0, 0)
    ts(pg, pi, 4, A.arith_shift_right)
    ts(pa, pi, 15, A.bitwise_and)
    ts(pp, pi, 4, A.arith_shift_right, 1, A.bitwise_and)
    pf, pgf, pg16, paf, od, ev, pa8 = [S("cols", b) for b in range(7)]
    tc(od, pp)
    ts(ev, pp, -1.0, A.mult, 1.0, A.add)
    ts(pg16, pg, 16.0, A.mult)
    tc(pf, pi)
    tc(pgf, pg)
    tc(paf, pa)
    ts(pa8, pa, 8.0, A.mult)
    ts(v("ID"), v("ROWI", 15, 143), pf, A.is_equal)
    ts(v("IDM"), v("ROWI", 15, 143), pf, A.is_equal, float(-BIG), A.mult)
    ts(v("IDH"), v("ID"), float(-BIG // 2), A.mult)
    ts(v("IDN"), v("ID"), -1.0, A.mult)
    for nm, wv in (("WB1", 1.0), ("WBK", 16384.0), ("WB4", 4.0), ("WBM", -2.0)):
        ts(v(nm), v("ROWI"), pg16, A.is_equal, wv, A.mult)
    for t in range(ST):
        ms(v("W%d" % t, 256 + 8 * t, 264 + 8 * t), -BIG)
        if t:
            ms(v("R%d" % t, 256 + 8 * t, 264 + 8 * t), 64.0)
    ms(v("X", 4096, NX), 0.0)
    ms(v("ZERO"), 0.0)
    ms(v("XB", 0, 8), 0.0)
    ms(v("ONES"), 1.0)

    def turn(raw, w0, w1):
        for b in range(8):
            tp(v("TA", b, 256, 8), v(raw, b, 256, 8))
            tp(v("TB", b, 256, 8), v("RU", b, 256, 8))
        ts(v("TC", 0, 128), v("TA", 0, 128), ev, A.mult)
        ts(v("TC", 128, 256), v("TB", 0, 128), ev, A.mult)
        ts(v("TE", 0, 128), v("TB", 128, 256), od, A.mult)
        ts(v("TE", 128, 256), v("TA", 128, 256), od, A.mult)
        tt(w0, v("TC", 0, 128), v("TE", 0, 128), A.add)
        tt(w1, v("TC", 128, 256), v("TE", 128, 256), A.add)

    ts(v("OUT"), v("VR"), 4096.0, A.mult, float(-BIG), A.add)
    tt(v("RT", 0, 128), v("OUT", 0, 256, 2), v("CR", 0, 256, 2), A.add)
    tt(v("RT", 128, 256), v("OUT", 1, 256, 2), v("CR", 1, 256, 2), A.add)
    tc(v("RU", 0, 128), v("RT", 128, 256))
    tc(v("RU", 128, 256), v("RT", 0, 128))
    turn("RT", v("W0", 0, 128), v("W0", 128, 256))

    def lists(t):
        P = 32 + t
        W = "W%d" % t
        for r0, r1 in ((0, 9), (9, P)):
            ts(v("VI", r0 * 8, r1 * 8), v(W, r0 * 8, r1 * 8), 12, A.arith_shift_right, 4095, A.bitwise_and)
            tc(v("VL", r0 * 8, r1 * 8), v("VI", r0 * 8, r1 * 8))
        ts(v("CI", 0, P * 8 - 16), v(W, 0, P * 8 - 16), 4095, A.bitwise_and)
        tc(v("CL", 0, P * 8 - 16), v("CI", 0, P * 8 - 16))

    def late_constants():
        ts(S("wt", 0), v("WT"), 1.0, A.mult)
        ts(v("WBW"), v("WB1"), S("wt", 0), A.mult)
        ts(v("CIO"), v("CIO"), 4, A.arith_shift_right)
        ts(v("BLK"), v("CIO"), pgf, A.is_equal)
        ts(v("DG"), v("ROWI", 15, 31), paf, A.is_equal, 128.0, A.mult)
        ts(v("POS"), v("POS"), paf, A.add)
        ts(S("BA"), S("BA"), paf, A.add)
        ts(S("II"), S("B8"), pa8, A.add)
        ts(S("DUMP"), S("II"), 4096.0, A.add)
        ts(S("KF0"), S("II"), 1.0 / 128, A.mult)
        tt(S("KF"), S("KF0"), S("DUMP"), A.add)
        tt(S("V00"), v("VI", 0, 8), S("DUMP"), A.subtract)
        ts(v("GB", 0, 128, 1, 0, 8), v("CIO", 0, 128, 1, 0, 8), v("SM", pf[1], pf[2], 1, 0, 8), A.is_equal)
        thf = v("SM", scol["wt"] + 1, scol["wt"] + 2, 1, 0, 8)
        tc(thf, v("THR8"))
        mm(v("pS", 0, 1), v("GB", 0, 128, 1, 0, 8), thf, True, True)
        tc(S("th", 0), v("pS", 0, 1))
        tc(S("lim", 0), S("th", 0))

    def scalar_constants():
        act(S("THR"), S("II"), AF.Copy, bias=-0.5, scale=0.5)
        act(S("HC"), S("II"), AF.Copy, bias=0.5, scale=0.5)
        act(S("HI"), S("II"), AF.Copy, scale=0.5)
        act(S("KD"), S("KF"), AF.Copy, scale=128.0)
        for b in range(8):
            act(v("EXC", b * 16, b * 16 + 16), v("DG"), AF.Copy, scale=S("KF", b))
        tt(S("HK"), S("HC"), S("KD"), A.subtract)

    def masks(t):
        R, G8 = "R%d" % t, (30 + t) * 8
        mm(v("pI", 0, G8), v("ID"), v(R, 8, G8 + 8), True, False)
        mm(v("pI", 0, G8), v("IDN"), v(R, 0, G8), False, True)
        act(S("b25"), S("n%d" % t), AF.Copy, bias=2.5, scale=-1.0)
        for b in range(8):
            act(v("INV", b, G8, 8), v(R, b, G8, 8), AF.Sign, bias=S("b25", b))
        act(v("MK", 0, G8), v("pI", 0, G8), AF.Relu, bias=1.0, scale=-1.0)

    def dedupe(t2):
        mm(v("pI", 0, 128), v("BLK"), v("EXC"), True, False)
        for b in range(8):
            act(v("EX", b * 16, b * 16 + 16), v("DG"), AF.Copy, scale=v("SM", t2[1] + b, t2[1] + b + 1))
        mm(v("pI", 0, 128), v("BLK"), v("EX"), False, True)
        ts(S("nc0"), t2, -128.0, A.mult)
        tt(S("nc"), S("nc0"), S("HK"), A.add)

    def far(b):
        act(v("AA", b * 128, b * 128 + 128), v("pI", 0, 128), AF.Abs, bias=S("nc", b))

    def hit(b):
        x, o = v("AA", b * 128, b * 128 + 128), v("AB", b * 128, b * 128 + 128)
        emit("a", lambda: g.scalar.activation(ap(o), ap(x), AF.Relu, bias=ap(S("HI", b)), scale=-1.0, accum_out=ap(S("hit", b))),
             [o, S("hit", b)], [x, S("HI", b)], cost=0.126)

    def half(nm, k):
        c = S(nm)[1]
        return v("SM", c + NV * k, c + (8 if k else NV))

    def dedupe2(t2, off):
        for b in range(NV):
            tr(S("mn", b), v("AA", b * 128, b * 128 + 128), A.min)
        tt(half("nd", 0), half("mn", 0), half("THR", 0), A.is_gt)
        ts(half("nd", 1), half("hit", 1), 0.0, A.is_equal)
        tt(S("t3"), t2, S("nd"), A.mult)
        tt(S("t4"), S("t3"), S("DUMP"), A.add)
        tc(v(off), S("t4"))

    xwin = v("X")

    def step(t):
        P = 32 + t
        P1, G = P + 1, P - 2
        n8, m8, G8 = P * 8, P1 * 8, G * 8
        W, R, Wn, Rn = "W%d" % t, "R%d" % t, "W%d" % (t + 1), "R%d" % (t + 1)
        YR, M, LW, LY, LM = ["%s%d" % (k, t) for k in ("YR", "M", "LW", "LY", "LM")]
        n, nn, V0, V0n, TH = S("n%d" % t), S("n%d" % (t + 1)), S("V0%d" % t), S("V0%d" % (t + 1)), S("lim", t)
        d = 1 + t % 5
        to, fr = T.cores[(rank + d) % N], T.cores[(rank - d) % N]
        ne = len(topo.engines(fr, core))
        for buf, sem, wd in ((LW, "aw", m8), (LY, "ay", 128 + m8), (LM, "am", 24)):
            record((sem + str(t), ne), [v(buf, 0, wd)], [], {})

        c1, c2, c3 = GCS
        gc = [(0, c1), (c1, c2), (c2, c3), (c3, G)]
        vc = [(0, c1 + 1), (c1 + 1, c2 + 1), (c2 + 1, c3 + 1), (c3 + 1, P)]

        def gv(c):
            r0, r1 = vc[c]
            for r0, r1 in ([(0, 5), (5, r1)] if c == 0 else [(r0, r1)]):
                act(v("XV", r0 * 128, r1 * 128), ind(v("X", 0, 4096), v("VL", r0 * 8, r1 * 8)), AF.Copy, scale=0.5)

        def hs(c):
            r0, r1 = gc[c]
            return [(r, min(r + 4, r1)) for r in range(r0, r1, 4)]

        hb = ("pA", "pB", "pJ")

        def idp(c):
            for k, (r0, r1) in enumerate(hs(c)):
                mm(v(hb[k], 0, (r1 - r0) * 128), v("ID"), v("XV", r0 * 128, r1 * 128), True, r0 < HA)
                if r0 >= HA:
                    mm(v(hb[k], 0, (r1 - r0) * 128), v("ID"), v("XV", r0 * 128 + 128, r1 * 128 + 128), False, True)

        def hh(c):
            for k, (r0, r1) in enumerate(hs(c)):
                if r0 >= HA:
                    act(v("H", r0 * 128, r1 * 128), v(hb[k], 0, (r1 - r0) * 128), AF.Copy)
                    continue
                tt(v("H", r0 * 128, r1 * 128), v("XV", r0 * 128 + 128, r1 * 128 + 128), v(hb[k], 0, (r1 - r0) * 128), A.add)

        def dd(c):
            r0, r1 = gc[c]
            tt(v("D", r0 * 128, r1 * 128), ind(v("X", 0, 4096), v("CL", r0 * 8, r1 * 8)), v("H", r0 * 128, r1 * 128), A.subtract)

        def aba(c):
            r0, r1 = gc[c]
            act(v("AB", r0 * 128, r1 * 128), v("D", r0 * 128, r1 * 128), AF.Abs)

        def sums(bank, wb, buf, r0, r1, last):
            for a in range(16):
                mm(v(bank, r0 * 8, r1 * 8), v(wb, 15 - a, 143 - a), v(buf, r0 * 128 + a, r1 * 128, 16), False, last and a == 15)

        gv(0)
        if t == 0:
            masks(0)
            late_constants()
        ts(S("L"), n, 4.0, A.is_ge)
        tt(S("nL"), n, S("L"), A.mult)
        idp(0)
        mm(v("pK", 0, G8), v("ID"), v("QT", 0, G8), True, False)
        mm(v("pK", 0, G8), v("ID"), v(R, 0, G8), False, False)
        mm(v("pK", 0, G8), v("IDH"), v("ONES", 0, G8), False, False)
        mm(v("pK", 0, G8), v("IDH"), v("INV", 0, G8), False, False)
        mm(v("pK", 0, G8), v("IDM"), v("MK", 0, G8), False, False)
        mm(v("pD", 0, n8), v("ID"), v("ZERO", 0, n8), True, False)
        gv(1)
        gv(2)
        hh(0)
        dd(0)
        idp(1)
        sums("pD", "WBM", "XV", 0, c1 + 1, False)
        hh(1)
        idp(2)
        sums("pD", "WBM", "XV", c1 + 1, c2 + 1, False)
        aba(0)
        sums("pK", "WBK", "AB", 0, c1, False)
        gv(3)
        dd(1)
        hh(2)
        idp(3)
        sums("pD", "WBM", "XV", c2 + 1, c3 + 1, False)
        aba(1)
        sums("pK", "WBK", "AB", c1, c2, False)
        dd(2)
        hh(3)
        aba(2)
        sums("pK", "WBK", "AB", c2, c3, False)
        dd(3)
        aba(3)
        sums("pK", "WBK", "AB", gc[3][0], G, True)
        sums("pD", "WBM", "XV", c3 + 1, P, False)
        tt(v("pJ", 8, m8), v(W, 0, n8), v(W, 8, m8), A.subtract)
        if t:
            cj = v("SI", 236, 237)
            tc(cj, v("pS", 400, 401))
            ts(cj, cj, 31, A.bitwise_and)
            tt(TH, S("th", 0), cj, A.add)
        ts(v("Z0", 0, G8), v("VI", 0, G8), 4096.0, A.mult, float(-BIG), A.add)
        tt(v("Z", 0, G8), v("Z0", 0, G8), v("VI", 8, G8 + 8), A.add)
        if t == 0:
            scalar_constants()

        for b in range(8):
            tr(v("SI", J("mx")[1] + b, J("mx")[1] + b + 1), v("pK", b, G8, 8), A.max)
        ts(J("q"), J("mx"), 8064, A.bitwise_and)
        tt(S("jk"), S("BA"), J("q"), A.subtract)
        tc(v("JL"), S("jk"))
        tc(v("DK"), ind(v("D", 0, G * 128), v("JL")))
        tt(v("TK"), ind(v("H", 0, G * 128), v("JL")), v("DK"), A.subtract)
        Y = v(YR, 0, 128)
        ts(Y, v("TK"), 0.0, A.max, 63.0, A.min)
        for k in range(2):
            ts(v("pY", k * 128, k * 128 + 128), Y, 0.5, A.mult)
        ts(J("k"), J("mx"), 127, A.bitwise_and)
        tc(S("k"), J("k"))
        ts(S("bO"), J("mx"), -1.0 / 128, A.mult, 0.5, A.add)
        act(S("nk"), S("k"), AF.Copy, bias=-1.0, scale=-1.0)
        act(S("k15"), S("k"), AF.Copy, bias=1.5)
        act(S("kn"), S("k"), AF.Copy, scale=-1.0)
        act(v(M, 16, 24), S("L"), AF.Copy)
        act(S("jb"), S("jk"), AF.Copy, bias=-0.5, scale=-1.0)
        act(S("jb1"), S("jk"), AF.Copy, bias=-128.0, scale=-1.0)
        for b in range(8):
            act(v(YR, 128 + b, 128 + m8, 8), v(R, b, m8, 8), AF.Relu, bias=S("nk", b))
        send(W, LW, m8, "aw%d" % t, to)
        send(YR, LY, 128 + m8, "ay%d" % t, to)
        for b in range(8):
            act(v("pA", b, n8, 8), v(R, b, n8, 8), AF.Relu, bias=S("k15", b), scale=-1.0)
        for b in range(8):
            act(v("RQ", b, n8, 8), v(R, b, n8, 8), AF.Relu, bias=S("nL", b), scale=-1.0)
        for b in range(8):
            act(v("pB", b, G8, 8), v("pK", b, G8, 8), AF.Sign, bias=S("bO", b), scale=1.0 / 128)

        for a in range(16):
            mm(v("pS", 304, 312), v("WB1", 15 - a, 143 - a), v(YR, a, 128, 16), a == 0, a == 15)
        dc = [(2, 8), (8, 16), (16, 24), (24, P)]
        for c, (r0, r1) in enumerate(dc):
            for r in range(r0, r1, 2):
                e = min(r + 2, r1)
                tt(v("AB", r * 128, e * 128), v("XV", r * 128, e * 128), v("pY", 0, (e - r) * 128), A.max)
            sums("pD", "WB4", "AB", r0, r1, c == 3)
            if c == 1:
                ts(S("lm"), v("pS", 304, 312), TH, A.add)
                for b in range(8):
                    act(v("LX", b, n8, 8), v("pA", b, n8, 8), AF.Identity, bias=S("lm", b), scale=-8192.0)
                for b in range(8):
                    act(v("SP", b, m8, 8), v("POS", b, m8, 8), AF.Sign, bias=S("jb", b))
                for b in range(8):
                    act(v("OA", b, m8, 8), v("POS", b, m8, 8), AF.Abs, bias=S("jb1", b))
                act(v("OA", 0, m8), v("OA", 0, m8), AF.Relu, bias=1.0, scale=-1.0)
                for b in range(8):
                    act(v("A2", b, m8, 8), v(R, b, m8, 8), AF.Relu, bias=S("k", b), scale=-1.0)
        for a in range(16):
            mm(v("pI", 0, 8), v("WBW", 15 - a, 143 - a), v(YR, a, 128, 16), a == 0, a == 15)
        mm(v("pY", 8, m8), v("ID"), v("ONES", 8, m8), True, False)
        mm(v("pY", 8, m8), v("ID"), v(R, 0, n8), False, False)
        mm(v("pY", 8, m8), v("IDN"), v(R, 8, m8), False, True)
        tt(S("nk1"), n, S("nk"), A.add)
        tt(v("PZ", 0, G8), v("pB", 0, G8), v("Z", 0, G8), A.mult)
        for b in range(8):
            tr(v("SI", J("z")[1] + b, J("z")[1] + b + 1), v("PZ", b, G8, 8), A.min)
        ts(J("vk"), J("z"), 12, A.arith_shift_right, 4095, A.bitwise_and)
        ts(J("vk1"), J("z"), 4095, A.bitwise_and)
        tt(v(M, 8, 16), J("vk1"), S("DUMP"), A.subtract)
        tt(v("pA", 0, n8), v("pD", 0, n8), v("LX", 0, n8), A.is_le)
        tt(v("PZ", 0, n8), v("pA", 0, n8), v("RQ", 0, n8), A.mult)
        for b in range(8):
            tr(S("vm", b), v("PZ", b, n8, 8), A.max)
        ts(S("cl"), S("vm"), 0.0, A.is_gt)
        tt(S("sz0"), S("cl"), S("nk1"), A.mult)
        tt(v(M, 0, 8), S("sz0"), S("vm"), A.subtract)
        sz = v(M, 0, 8)
        send(M, LM, 24, "am%d" % t, to)
        tt(S("gr"), S("L"), S("cl"), A.subtract)
        for b in range(8):
            act(v("GG", b, m8, 8), v("SP", b, m8, 8), AF.Relu, scale=S("gr", b))

        tc(J("u"), v("pI", 0, 8))
        ts(J("u2"), J("u"), 4095, A.bitwise_and)
        tt(J("uu"), J("u2"), J("u2"), A.mult)
        ts(J("v37"), J("vk"), 37.0, A.mult)
        ts(J("us"), J("uu"), 5, A.arith_shift_right)
        tt(J("h0"), J("us"), J("v37"), A.add)
        ts(J("h"), J("h0"), 4095, A.bitwise_and)
        tt(S("hd"), J("h"), S("DUMP"), A.subtract)
        tt(S("t2g"), S("hd"), S("gr"), A.mult)
        dedupe(S("t2g"))
        ts(S("wn0"), J("h"), 4096.0, A.mult, float(-BIG), A.add)
        tt(S("wn1"), S("wn0"), J("vk"), A.add)
        tt(S("wn"), S("wn1"), S("gr"), A.mult)
        for b in range(8):
            act(v("pD", b, m8, 8), v("OA", b, m8, 8), AF.Copy, scale=S("wn", b))
        tt(v("XB", 8, m8), v("GG", 8, m8), v("pY", 8, m8), A.mult)
        mm(v("pA", 0, m8), v("ID"), v(R, 0, m8), True, False)
        mm(v("pA", 0, m8), v("ID"), v("XB", 0, m8), False, True)
        tt(v("pB", 8, m8), v("GG", 8, m8), v("pJ", 8, m8), A.mult)
        tt(v("WA", 8, m8), v(W, 8, m8), v("pB", 8, m8), A.add)
        tc(v("WA", 0, 8), v(W, 0, 8))
        tt(S("kns"), S("kn"), sz, A.subtract)
        tt(S("zl"), J("z"), S("L"), A.mult)
        act(v("YX", 0, 8), S("cl"), AF.Copy)
        act(S("rest"), S("L"), AF.Copy, bias=1.0, scale=-1.0)
        for b in range(8):
            far(b)
        for b in range(NV, 8):
            hit(b)
        for b in range(8):
            act(v("A1", b, m8, 8), v("pA", b, m8, 8), AF.Relu, bias=S("kns", b))
        tt(S("ng"), n, S("gr"), A.add)
        ts(S("ng"), S("ng"), 32.0, A.min)
        tt(S("n2"), S("ng"), sz, A.subtract)
        dedupe2(S("t2g"), "OL")
        tc(ind(xwin, v("OL")), Y)
        mm(v("pA", 0, m8), v("ID"), v("A1", 0, m8), True, False)
        mm(v("pA", 0, m8), v("IDN"), v("A2", 0, m8), False, True)
        act(v("RQ", 0, m8), v("pA", 0, m8), AF.Abs)
        act(v("RQ", 0, m8), v("RQ", 0, m8), AF.Relu, bias=1.0, scale=-1.0)
        mm(v("pS", 0, m8), v("ID"), v(LY, 128, 128 + m8), True, False)
        mm(v("pS", 0, m8), v("IDN"), v(R, 0, m8), False, True)
        if t < ST - 1:
            for b in range(8):
                mm(v("pS", 400, 401), v("ONES", 0, 128), v("YX", b, b + 1), b == 0, b == 7)

        tt(S("rc"), v(LM, 0, 8), S("rest"), A.mult)
        tt(S("dv"), v(LM, 8, 16), V0, A.subtract)
        tt(S("tk"), S("rc"), S("n2"), A.is_gt)
        tt(nn, S("rc"), S("n2"), A.max)
        tt(S("dvt"), S("dv"), S("tk"), A.mult)
        tt(S("has"), nn, v(LM, 16, 24), A.min)
        tt(V0n, V0, S("dvt"), A.add)
        tt(S("t2b"), V0n, S("has"), A.mult)
        dedupe(S("t2b"))
        for b in range(8):
            act(v("T1", b, m8, 8), v("RQ", b, m8, 8), AF.Copy, scale=S("zl", b))
        for b in range(8):
            act(v("RX", b, m8, 8), v("pA", b, m8, 8), AF.Identity, bias=S("k", b))
        for b in range(8):
            ts(v("pK", b, m8, 8), v(LW, b, m8, 8), S("tk", b), A.mult)
        tt(v("TM", 0, m8), v("T1", 0, m8), v("pD", 0, m8), A.add)
        tt(v("TM", 0, m8), v("TM", 0, m8), v("pK", 0, m8), A.add)
        ts(v("pY", 0, m8), v("TM", 0, m8), 0.0, A.is_equal)
        tt(v("pB", 0, m8), v("WA", 0, m8), v("pY", 0, m8), A.mult)
        tt(v(Wn, 0, m8), v("TM", 0, m8), v("pB", 0, m8), A.add)
        for b in range(8):
            far(b)
        for b in range(NV, 8):
            hit(b)
        for b in range(8):
            act(v("TDR", b, m8, 8), v("pS", b, m8, 8), AF.Copy, scale=S("tk", b))
        mm(v("pJ", 0, m8), v("ID"), v("RX", 0, m8), True, False)
        mm(v("pJ", 0, m8), v("ID"), v("TDR", 0, m8), False, True)
        act(v(Rn, 0, m8), v("pJ", 0, m8), AF.Copy)
        dedupe2(S("t2b"), "OB")
        tt(v("BS"), ind(xwin, v("OB")), v(LY, 0, 128), A.add)
        if t < ST - 1:
            masks(t + 1)
        else:
            mm(v("pA", 0, 280), v("ID"), v(Rn, 8, 288), True, False)
            mm(v("pA", 0, 280), v("IDN"), v(Rn, 0, 280), False, True)
            mm(v("pY", 0, 288), v("ID"), v("PP"), True, False)
            mm(v("pY", 0, 288), v("IDN"), v(Rn), False, True)
            act(S("n5"), nn, AF.Copy, bias=-0.5)
            for b in range(8):
                act(v("SP", b, 288, 8), v(Rn, b, 288, 8), AF.Sign, bias=S("n5", b), scale=-1.0)
            act(v("pB", 0, 288), v("SP"), AF.Relu)
            act(v("T1", 0, 280), v("pA", 0, 280), AF.Sign)
        ts(v("BO"), v("BS"), 0.5, A.mult, -0.25, A.add)
        tc(ind(xwin, v("OB")), v("BO"))
        if t < ST - 1:
            lists(t + 1)

    lists(0)
    tc(S("n0"), v("NR"))
    for t in range(ST):
        step(t)

    so = [dma("s", T.yx[:, 0:2048], ap(v("X", 0, 2048)), [], [v("X", 0, 2048)]),
          dma("a", T.yx[:, 2048:4096], ap(v("X", 2048, 4096)), [], [v("X", 2048, 4096)]),
          dma("s", T.yn[:], ap(S("n4")), [], [S("n4")])]
    ms(v("T1", 280, 288), 1.0)
    ts(v("U"), v("W4"), float(BIG), A.add)
    tt(v("E"), v("T1"), v("pB", 0, 288), A.mult)
    tt(v("DLT"), v("E"), v("pY", 0, 288), A.mult)
    tt(v("U"), v("U"), v("E"), A.mult)
    for i in range(6):
        lo = 8 << i
        w = 288 - lo
        ts(v("BIT", lo, 288), v("DLT", lo, 288), i, A.arith_shift_right, 1, A.bitwise_and)
        tc(v("pA", lo, 288), v("BIT", lo, 288))
        tt(v("pB", lo, 288), v("U", lo, 288), v("pA", lo, 288), A.mult)
        if i < 5:
            tt(v("pK", lo, 288), v("DLT", lo, 288), v("pA", lo, 288), A.mult)
        tt(v("U", lo, 288), v("U", lo, 288), v("pB", lo, 288), A.subtract)
        if i < 5:
            tt(v("DLT", lo, 288), v("DLT", lo, 288), v("pK", lo, 288), A.subtract)
        tt(v("U", 0, w), v("U", 0, w), v("pB", lo, 288), A.add)
        if i < 5:
            tt(v("DLT", 0, w), v("DLT", 0, w), v("pK", lo, 288), A.add)
    tc(v("RU", 0, 128), v("U", 128, 256))
    tc(v("RU", 128, 256), v("U", 0, 128))
    turn("U", v("OI", 0, 256, 2), v("OI", 1, 256, 2))
    ts(v("VI", 0, 256), v("OI"), 12, A.arith_shift_right)
    tc(v("OV"), v("VI", 0, 256))
    so.append(dma("s", T.yv[:], ap(v("OV")), [], [v("OV")]))
    ts(v("CI", 0, 256), v("OI"), 4095, A.bitwise_and)
    tc(v("OC"), v("CI", 0, 256))
    so.append(dma("a", T.yc[:], ap(v("OC")), [], [v("OC")]))
    flush()
    for s in so:
        g.sync.wait_ge(T.sem[s], 16)
    for s in ("qv", "qa", "qt", "qp"):
        g.sync.wait_ge(T.sem[s], cnt[s])
    g.wait_ge(T.sem.ls, cnt["ls"])
